import numpy as np
import ml_dtypes


def mxq(x, axis, fmt="e4m3"):
    dtype, down = {"e4m3": (ml_dtypes.float8_e4m3fn, 7), "e5m2": (ml_dtypes.float8_e5m2, 14)}[fmt]
    v = np.moveaxis(np.asarray(x, np.float32).astype(ml_dtypes.bfloat16).astype(np.float64), axis, -1)
    blocks = v.reshape(v.shape[:-1] + (-1, 32))
    amax = np.abs(blocks).max(-1, keepdims=True)
    byte = np.maximum(np.where(amax > 0, np.frexp(amax)[1] - 1 + 127, 0) - down, 1)
    scale = np.exp2(byte - 127.0)
    codes = (blocks / scale).astype(np.float32).astype(dtype).astype(np.float64)
    return np.moveaxis((codes * scale).reshape(v.shape), -1, axis)


WIDE = False


def mx_kscale(k):
    if not WIDE:
        return np.ones(k)
    levels = np.array([10, -10, 5, -5, 0])
    if k % 512:
        return np.exp2(np.random.permutation(np.resize(levels, k // 32))).repeat(32)
    a = np.empty((k // 512, 16))
    for p in range(k // 512):
        a[p, :8] = np.random.permutation(np.resize(levels, 8))
        for g in range(8):
            far = levels[np.abs(levels - a[p, g]) >= 10]
            a[p, g + 8] = far[np.random.randint(len(far))]
    return np.exp2(a.ravel()).repeat(32)


BF16 = ml_dtypes.bfloat16


def bf(x):
    return np.asarray(x, np.float32).astype(BF16)


def f64(x):
    return np.asarray(x).astype(np.float64)


E2M1 = np.array([0.0, 0.5, 1.0, 1.5, 2.0, 3.0, 4.0, 6.0, -0.0, -0.5, -1.0, -1.5, -2.0, -3.0, -4.0, -6.0])


def pack_weight(w, fmt):
    k, n = w.shape
    w = f64(bf(w)).reshape(k // 32, 32, n)
    amax = np.abs(w).max(1)
    if fmt == "e4m3":
        byte = np.frexp(amax)[1] - 1 + 127 - 7
    else:
        mant, ex = np.frexp(amax / 6.0)
        byte = np.where(mant > 0.5, ex, ex - 1) + 127
    byte = np.clip(np.where(amax > 0, byte, 1), 1, 254)
    scaled = (w * np.exp2(127.0 - byte)[:, None, :]).reshape(k, n).astype(np.float32)
    by_word = np.ascontiguousarray(scaled.reshape(k // 512, 128, 4, n).transpose(0, 1, 3, 2))
    if fmt == "e4m3":
        words = by_word.astype(ml_dtypes.float8_e4m3fn).view(np.uint8)
    else:
        c = by_word.astype(ml_dtypes.float4_e2m1fn).view(np.uint8) & 0xF
        words = c[..., 0::2] | (c[..., 1::2] << 4)
    return np.ascontiguousarray(words), np.ascontiguousarray(byte.astype(np.uint8).reshape(k // 512, 16, n))


def unpack_weight(words, scales, fmt):
    g, p, n, _ = words.shape
    if fmt == "e4m3":
        vals = np.ascontiguousarray(words).view(ml_dtypes.float8_e4m3fn).astype(np.float64)
    else:
        nib = np.empty((g, p, n, 4), np.uint8)
        nib[..., 0::2] = words & 0xF
        nib[..., 1::2] = words >> 4
        vals = E2M1[nib]
    vals = vals * np.repeat(np.exp2(scales.astype(np.float64) - 127.0), 8, axis=1)[..., None]
    return vals.transpose(0, 1, 3, 2).reshape(g * 512, n)
def pack4(w):
    words, scales = pack_weight(w, "e2m1")
    return words.reshape(words.shape[0], 128, -1), scales


def unpack4(words, scales):
    return unpack_weight(words.reshape(words.shape[0], 128, -1, 2), scales, "e2m1")


def planes(Y):
    n, m = Y.shape
    b = f64(bf(Y)).reshape(n // 32, 32, m)
    amax = np.abs(b).max(1)
    byte = np.clip(np.where(amax > 0, np.frexp(amax)[1] - 1 + 127 - 7, 1), 1, 254)
    codes = (b * np.exp2(127.0 - byte)[:, None, :]).reshape(n, m).astype(np.float32).astype(ml_dtypes.float8_e4m3fn).view(np.uint8)
    words = codes.reshape(n // 512, 128, 4, m).transpose(0, 1, 3, 2)
    return np.ascontiguousarray(words), np.ascontiguousarray(byte.astype(np.uint8).reshape(n // 512, 16, m))


T, CE, CM, S, P = 1024, 512, 512, 2048, 512
LAM = 0.5

def setup_inputs():
    se, sm, t = mx_kscale(CE), mx_kscale(CM), mx_kscale(S)
    lead = np.exp(0.4 * np.random.randn(1, S)) * np.random.randn(CE + CM, S) / np.sqrt(S)
    inverse = np.linalg.pinv(np.hstack([lead, LAM * np.eye(CE + CM)]))[:S].T
    weight = 1 / np.sum(inverse * inverse, axis=0)
    amp = np.exp(0.4 * np.random.randn(T, 1))
    eeg = amp * np.random.randn(T, CE)
    meg = amp * np.random.randn(T, CM)
    member = np.exp(2.0 * np.random.randn(S, P))
    member = member / np.sum(member, axis=0, keepdims=True)
    words, scales = pack4(inverse[:CE] / se[:, None])
    return {"eeg": bf(eeg * se), "meg": bf(meg * sm),
            "inv_eeg_words": words, "inv_eeg_scales": scales,
            "inv_meg": bf(inverse[CE:] / sm[:, None]),
            "source_weight": bf(weight * t),
            "parcel_weights": bf(member / t[:, None]),
            "power_scale": bf(np.exp(0.5 * np.random.randn(P))),
            "gain": bf(np.exp(0.8 * np.random.randn(P)))}

def reference(eeg, meg, inv_eeg_words, inv_eeg_scales, inv_meg, source_weight, parcel_weights, power_scale, gain):
    J = (mxq(f64(meg), 1, "e4m3") @ mxq(f64(inv_meg), 0, "e4m3")) + (mxq(f64(eeg), 1, "e4m3") @ unpack4(inv_eeg_words, inv_eeg_scales))
    D = J * J * f64(source_weight)
    R = mxq(D, 1, "e4m3") @ mxq(f64(parcel_weights), 0, "e4m3")
    y = np.log(1 + R * f64(power_scale)) * f64(gain)
    Y = y.T
    words, scales = planes(Y)
    return y, words, scales

@@ -1,0 +1,332 @@
+from contextlib import ExitStack
+
+import concourse.mybir as mybir
+from concourse.masks import make_identity
+
+T, C, S, NP = 1024, 512, 2048, 512
+FLOPS = 2 * T * (2 * C * S + S * NP)
+
+F32 = mybir.dt.float32
+BF16 = mybir.dt.bfloat16
+I32 = mybir.dt.int32
+U32 = mybir.dt.uint32
+U8 = mybir.dt.uint8
+FP8X4 = mybir.dt.float8_e4m3fn_x4
+FP4X4 = mybir.dt.float4_e2m1fn_x4
+ACT = mybir.ActivationFunctionType
+ALU = mybir.AluOpType
+
+P = 128
+HALF = 512
+GROUPS = S // 512
+
+
+def tile_minimum_norm_parcel_power_k6_kernel(
+    tc, eeg, meg, inv_eeg_words, inv_eeg_scales, inv_meg, source_weight, parcel_weights,
+    power_scale, gain, out_0, out_1, out_2
+):
+    nc = tc.nc
+    with ExitStack() as ctx:
+        sb = ctx.enter_context(tc.tile_pool(name="sb", bufs=1))
+        ps = ctx.enter_context(tc.psum_pool(name="ps", bufs=1))
+        ctx.enter_context(tc.manual_schedule())
+
+        def sbuf(name, shape, dtype):
+            return sb.tile(shape, dtype, name=name, align_bytes=64)
+
+        def staging(name):
+            return sb.tile([P, 2048], BF16, name=name, tag="grouped", bufs=5, align_bytes=64)
+
+        def bank(b, name, shape, dtype):
+            return ps.tile(shape, dtype, name=name, tag="bank%d" % b)
+
+        def quantize(name, grouped):
+            codes = sbuf(name + "_codes", [P, 512], U32)
+            scales = sbuf(name + "_scales", [P, 512], U8)
+            nc.vector.quantize_mx(out=codes[:].bitcast(FP8X4), scales=scales[:], in_=grouped[:])
+            return codes, scales
+
+        w_rows = sbuf("w_rows", [P, 512], BF16)
+        nc.vector.memset(w_rows[:], 0.0)
+        f_scales_raw = sbuf("f_scales_raw", [P, 512], I32)
+        nc.vector.memset(f_scales_raw[:], 0)
+        ident16 = sbuf("ident16", [P, P], BF16)
+        make_identity(nc, ident16[:])
+        ident32 = sbuf("ident32", [P, P], F32)
+        make_identity(nc, ident32[:])
+
+        def load_inv_meg(g):
+            raw = sbuf("inv_meg_raw%d" % g, [P, 4, 512], BF16)
+            nc.sync.dma_start(out=raw[:], in_=inv_meg[:, 512 * g:512 * (g + 1)].rearrange("(p j) n -> p j n", j=4))
+            return raw
+
+        def load_sensor(name, x, h):
+            raws = []
+            for a in range(2):
+                raw = sbuf("%s_raw%d%d" % (name, h, a), [P, 2 * C], BF16)
+                r0 = HALF * h + 256 * a
+                nc.sync.dma_start(out=raw[:], in_=x[r0:r0 + 256, :].rearrange("(p i) k -> p (i k)", i=2))
+                raws.append(raw)
+            return raws
+
+        def load_f_words(gg):
+            raw = sbuf("f_words_raw%d" % gg, [P, 512], I32)
+            nc.sync.dma_start(out=raw[:], in_=inv_eeg_words[0, :, 2048 * gg:2048 * (gg + 1)].bitcast(I32))
+            return raw
+
+        def load_parcel_weights(g):
+            raw = sbuf("pw_raw%d" % g, [P, 4, NP], BF16)
+            rows = parcel_weights[512 * g:512 * (g + 1), :].rearrange("(m t e) n -> t m e n", t=4, e=4)
+            for t in range(4):
+                nc.sync.dma_start(out=raw[:, t, :], in_=rows[t])
+            return raw
+
+        def load_parcel_vector(name, vec):
+            raw = sbuf(name, [P, 4], BF16)
+            nc.sync.dma_start(out=raw[:], in_=vec.rearrange("(p u) -> p u", u=4))
+            return raw
+
+        w_raw = sbuf("w_raw", [GROUPS, 512], BF16)
+        nc.sync.dma_start(out=w_raw[:], in_=source_weight.rearrange("(g s) -> g s", g=GROUPS))
+        meg_raw = {0: load_sensor("meg", meg, 0)}
+        im_raw = {0: load_inv_meg(0)}
+        eeg_raw = {0: load_sensor("eeg", eeg, 0)}
+        fw_raw = {0: load_f_words(0)}
+        for q in range(4):
+            nc.sync.dma_start(out=f_scales_raw[32 * q:32 * q + 4, :], in_=inv_eeg_scales[0, 4 * q:4 * q + 4, :].bitcast(I32))
+        im_raw[1] = load_inv_meg(1)
+        fw_raw[1] = load_f_words(1)
+        im_raw[2] = load_inv_meg(2)
+        meg_raw[1] = load_sensor("meg", meg, 1)
+        eeg_raw[1] = load_sensor("eeg", eeg, 1)
+        im_raw[3] = load_inv_meg(3)
+        ps_raw = load_parcel_vector("ps_raw", power_scale)
+        gain_cols = load_parcel_vector("gain_cols", gain)
+        pw_raw = [load_parcel_weights(g) for g in range(GROUPS)]
+
+        def interleave_inv_meg(g):
+            grouped = staging("inv_meg_grouped%d" % g)
+            nc.vector.tensor_copy(
+                out=grouped[:].rearrange("p (t m e j) -> p t m j e", t=4, e=4, j=4),
+                in_=im_raw[g][:].rearrange("p j (m t e) -> p t m j e", t=4, e=4))
+            return grouped
+
+        def interleave_parcel_weights(g):
+            grouped = staging("pw_grouped%d" % g)
+            nc.vector.tensor_copy(
+                out=grouped[:].rearrange("p (u m t) -> p m t u", u=4, t=4),
+                in_=pw_raw[g][:].rearrange("p t (m u) -> p m t u", u=4))
+            return grouped
+
+        def interleave(name, slots, copy=nc.vector.tensor_copy):
+            grouped = staging(name + "_grouped")
+            copy(
+                out=grouped[:].rearrange("p (c i t) -> p c t i", i=4, t=4),
+                in_=slots[:].rearrange("p t (c i) -> p c t i", i=4))
+            return grouped
+
+        def transpose_sensor(name, raw, first_bank):
+            banks = []
+            for a in range(2):
+                turned = bank(first_bank + a, "%s_turned%d" % (name, a), [P, 2, 2, P], F32)
+                for i in range(2):
+                    words = raw[a][:].bitcast(F32)
+                    for u in range(2):
+                        nc.tensor.transpose(turned[:, i, u, :], words[:, 256 * i + u:256 * (i + 1):2], ident32[:])
+                banks.append(turned)
+            return banks
+
+        def gather_sensor(name, banks):
+            grouped = sbuf(name + "_grouped", [P, 2048], BF16)
+            words = grouped[:].bitcast(F32).rearrange("p (a r i u) -> p a r i u", a=2, i=2, u=2)
+            for a in range(2):
+                nc.scalar.copy(out=words[:, a], in_=banks[a][:].rearrange("p i u r -> p r i u"))
+            return grouped
+
+        f_words = sbuf("f_words", [P, 4096], U8)
+        f_scales = sbuf("f_scales", [P, 2048], U8)
+
+        def sort_f_words(gg):
+            nc.vector.tensor_copy(
+                out=f_words[:, 2048 * gg:2048 * (gg + 1)].bitcast(I32).rearrange("p (g t m w) -> p g t m w", g=2, t=4, w=2),
+                in_=fw_raw[gg][:].rearrange("p (g m t w) -> p g t m w", g=2, t=4, w=2))
+
+        def meg_pass(h, g, t):
+            cur = bank(4 + t, "j%d%d%d" % (h, g, t), [P, HALF], F32)
+            codes, scales = im_q[g]
+            cols = slice(P * t, P * (t + 1))
+            nc.tensor.matmul_mx(
+                out=cur[:], lhsT=codes[:, cols].bitcast(FP8X4), lhsT_scale=scales[:, cols],
+                rhs=meg_q[h][0][:].bitcast(FP8X4), rhs_scale=meg_q[h][1][:], start=True, stop=False)
+            return cur
+
+        def eeg_pass(h, g, t, cur):
+            c0 = 512 * g + P * t
+            nc.tensor.matmul_mx(
+                out=cur[:], lhsT=f_words[:, 2 * c0:2 * (c0 + P)].bitcast(FP4X4), lhsT_scale=f_scales[:, c0:c0 + P],
+                rhs=eeg_q[h][0][:].bitcast(FP8X4), rhs_scale=eeg_q[h][1][:], start=False, stop=True)
+
+        def square(h, g, t, cur):
+            nc.scalar.activation(out=d_slots[h, g][:, t, :], in_=cur[:], func=ACT.Square, scale=root_w[:, 4 * t + g:4 * t + g + 1])
+
+        def currents(h, g):
+            d_slots[h, g] = sbuf("d_slots%d%d" % (h, g), [P, 4, HALF], BF16)
+            for t in range(4):
+                cur = meg_pass(h, g, t)
+                eeg_pass(h, g, t, cur)
+                square(h, g, t, cur)
+
+        def parcels(h, g):
+            codes, scales = pw_q[g]
+            for u in range(4):
+                if g == 0:
+                    r_banks[h, u] = bank(4 * h + u, "r%d%d" % (h, u), [P, HALF], F32)
+                cols = slice(P * u, P * (u + 1))
+                nc.tensor.matmul_mx(
+                    out=r_banks[h, u][:], lhsT=codes[:, cols].bitcast(FP8X4), lhsT_scale=scales[:, cols],
+                    rhs=d_q[h, g][0][:].bitcast(FP8X4), rhs_scale=d_q[h, g][1][:],
+                    start=(g == 0), stop=(g == GROUPS - 1))
+
+        def logarithm(h):
+            logs[h] = sbuf("logs%d" % h, [P, 4, HALF], F32)
+            for u in range(4):
+                nc.scalar.activation(out=logs[h][:, u, :], in_=r_banks[h, u][:], func=ACT.Ln, scale=ps_cols[:, u:u + 1], bias=1.0)
+
+        def apply_gain(h):
+            y_slots[h] = sbuf("y_slots%d" % h, [P, 4, HALF], F32)
+            for u in range(4):
+                nc.vector.tensor_scalar(out=y_slots[h][:, u, :], in0=logs[h][:, u, :], scalar1=gain_cols[:, u:u + 1], scalar2=None, op0=ALU.mult)
+
+        def transpose_y(h):
+            for i in range(4):
+                y_banks[h, i] = bank(i, "yt%d%d" % (h, i), [P, 4, P], F32)
+            for u in range(4):
+                for i in range(4):
+                    nc.tensor.transpose(y_banks[h, i][:, u, :], y_slots[h][:, u, P * i:P * (i + 1)], ident32[:])
+
+        def store_y(h, i, on_vector):
+            rows = sbuf("y_rows%d%d" % (h, i), [P, NP], F32)
+            src = y_banks[h, i][:].rearrange("p u m -> p m u")
+            dst = rows[:].rearrange("p (m u) -> p m u", u=4)
+            if on_vector:
+                nc.vector.tensor_copy(out=dst, in_=src)
+            else:
+                nc.scalar.copy(out=dst, in_=src)
+            r0 = HALF * h + P * i
+            nc.sync.dma_start(out=out_0[r0:r0 + P, :], in_=rows[:])
+
+        def store_planes(h, codes, scales):
+            cols = slice(HALF * h, HALF * (h + 1))
+            nc.sync.dma_start(out=out_1[0, :, cols, :].rearrange("p m t -> p (m t)").bitcast(I32), in_=codes[:].bitcast(I32))
+            for q in range(4):
+                nc.sync.dma_start(out=out_2[0, 4 * q:4 * q + 4, cols].bitcast(I32), in_=scales[32 * q:32 * q + 4, :].bitcast(I32))
+
+        im_q, meg_q, eeg_q, pw_q, d_q = {}, {}, {}, {}, {}
+        d_slots, r_banks, logs, y_slots, y_banks = {}, {}, {}, {}, {}
+
+        nc.vector.tensor_copy(
+            out=w_rows[0:GROUPS, :].rearrange("g (t m e) -> g t m e", t=4, e=4),
+            in_=w_raw[:].rearrange("g (m t e) -> g t m e", t=4, e=4))
+        w_turned = bank(7, "w_turned", [P, 4, P], BF16)
+        for t in range(4):
+            nc.tensor.transpose(w_turned[:, t, :], w_rows[:, P * t:P * (t + 1)], ident16[:])
+        root0 = sbuf("root0", [P, 4, GROUPS], F32)
+        w_cols = sbuf("w_cols", [P, 4, GROUPS], F32)
+        nc.scalar.activation(out=root0[:], in_=w_turned[:, :, 0:GROUPS], func=ACT.Sqrt)
+        nc.scalar.copy(out=w_cols[:], in_=w_turned[:, :, 0:GROUPS])
+        inv_root = sbuf("inv_root", [P, 16], F32)
+        nc.vector.reciprocal(out=inv_root[:], in_=root0[:].rearrange("p t g -> p (t g)"))
+
+        meg_grouped = gather_sensor("meg0", transpose_sensor("meg0", meg_raw[0], 0))
+        eeg_grouped = gather_sensor("eeg0", transpose_sensor("eeg0", eeg_raw[0], 2))
+        grouped = interleave_inv_meg(0)
+        half_quot = sbuf("half_quot", [P, 16], F32)
+        nc.vector.scalar_tensor_tensor(
+            out=half_quot[:], in0=w_cols[:].rearrange("p t g -> p (t g)"), scalar=0.5, in1=inv_root[:], op0=ALU.mult, op1=ALU.mult)
+        im_q[0] = quantize("inv_meg0", grouped)
+        meg_q[0] = quantize("meg0", meg_grouped)
+        root_w = sbuf("root_w", [P, 16], F32)
+        nc.vector.scalar_tensor_tensor(
+            out=root_w[:], in0=root0[:].rearrange("p t g -> p (t g)"), scalar=0.5, in1=half_quot[:], op0=ALU.mult, op1=ALU.add)
+        sort_f_words(0)
+        nc.vector.tensor_copy(
+            out=f_scales[:].bitcast(I32).rearrange("p (g t m) -> p g t m", g=GROUPS, t=4),
+            in_=f_scales_raw[:].rearrange("p (g m t) -> p g t m", g=GROUPS, t=4))
+        eeg_q[0] = quantize("eeg0", eeg_grouped)
+
+        d_slots[0, 0] = sbuf("d_slots00", [P, 4, HALF], BF16)
+        first = [meg_pass(0, 0, t) for t in range(4)]
+        for t in range(4):
+            eeg_pass(0, 0, t, first[t])
+            square(0, 0, t, first[t])
+
+        grouped = interleave_inv_meg(1)
+        sort_f_words(1)
+        im_q[1] = quantize("inv_meg1", grouped)
+        currents(0, 1)
+
+        grouped = interleave_inv_meg(2)
+        d_grouped = interleave("d00", d_slots[0, 0])
+        im_q[2] = quantize("inv_meg2", grouped)
+        d_q[0, 0] = quantize("d00", d_grouped)
+        meg_grouped = gather_sensor("meg1", transpose_sensor("meg1", meg_raw[1], 0))
+        eeg_grouped = gather_sensor("eeg1", transpose_sensor("eeg1", eeg_raw[1], 2))
+        currents(0, 2)
+
+        grouped = interleave_inv_meg(3)
+        meg_q[1] = quantize("meg1", meg_grouped)
+        im_q[3] = quantize("inv_meg3", grouped)
+        eeg_q[1] = quantize("eeg1", eeg_grouped)
+        ps_cols = sbuf("ps_cols", [P, 4], F32)
+        nc.scalar.copy(out=ps_cols[:], in_=ps_raw[:])
+        currents(0, 3)
+
+        def prepare(pw_g, d_hg):
+            a = interleave_parcel_weights(pw_g)
+            b = interleave("d%d%d" % d_hg, d_slots[d_hg])
+            pw_q[pw_g] = quantize("pw%d" % pw_g, a)
+            d_q[d_hg] = quantize("d%d%d" % d_hg, b)
+
+        prepare(0, (0, 1))
+        currents(1, 0)
+        prepare(1, (0, 2))
+        currents(1, 1)
+        parcels(0, 0)
+        prepare(2, (0, 3))
+        currents(1, 2)
+        parcels(0, 1)
+        prepare(3, (1, 0))
+        currents(1, 3)
+        last = interleave("d13", d_slots[1, 3], nc.scalar.copy)
+        parcels(0, 2)
+        parcels(0, 3)
+        logarithm(0)
+
+        a = interleave("d11", d_slots[1, 1])
+        b = interleave("d12", d_slots[1, 2])
+        d_q[1, 1] = quantize("d11", a)
+        parcels(1, 0)
+        parcels(1, 1)
+        apply_gain(0)
+        d_q[1, 2] = quantize("d12", b)
+        d_q[1, 3] = quantize("d13", last)
+        parcels(1, 2)
+        transpose_y(0)
+        parcels(1, 3)
+        y_grouped = interleave("y0", y_slots[0])
+        for i in range(2):
+            store_y(0, i, False)
+        logarithm(1)
+        store_y(0, 2, True)
+        y_q = quantize("y0", y_grouped)
+        store_y(0, 3, False)
+        store_planes(0, *y_q)
+        apply_gain(1)
+        transpose_y(1)
+        y_grouped = interleave("y1", y_slots[1])
+        store_y(1, 0, False)
+        store_y(1, 1, False)
+        y_q = quantize("y1", y_grouped)
+        store_y(1, 2, False)
+        store_planes(1, *y_q)
+        store_y(1, 3, True)

@@ -44,7 +44,7 @@ def tile_minimum_norm_parcel_power_k6_kernel(
             codes = sbuf(name + "_codes", [P, 512], U32)
             scales = sbuf(name + "_scales", [P, 512], U8)
             nc.vector.quantize_mx(out=codes[:].bitcast(FP8X4), scales=scales[:], in_=grouped[:])
-            return codes, scales
+            return codes[:], scales[:]
 
         w_rows = sbuf("w_rows", [P, 512], BF16)
         nc.vector.memset(w_rows[:], 0.0)
@@ -69,9 +69,9 @@ def tile_minimum_norm_parcel_power_k6_kernel(
                 raws.append(raw)
             return raws
 
-        def load_f_words(gg):
-            raw = sbuf("f_words_raw%d" % gg, [P, 512], I32)
-            nc.sync.dma_start(out=raw[:], in_=inv_eeg_words[0, :, 2048 * gg:2048 * (gg + 1)].bitcast(I32))
+        def load_f_words(g0, g1):
+            raw = sbuf("f_words_raw%d" % g0, [P, 256 * (g1 - g0)], I32)
+            nc.sync.dma_start(out=raw[:], in_=inv_eeg_words[0, :, 1024 * g0:1024 * g1].bitcast(I32))
             return raw
 
         def load_parcel_weights(g):
@@ -88,41 +88,41 @@ def tile_minimum_norm_parcel_power_k6_kernel(
 
         w_raw = sbuf("w_raw", [GROUPS, 512], BF16)
         nc.sync.dma_start(out=w_raw[:], in_=source_weight.rearrange("(g s) -> g s", g=GROUPS))
-        meg_raw = {0: load_sensor("meg", meg, 0)}
         im_raw = {0: load_inv_meg(0)}
+        meg_raw = {0: load_sensor("meg", meg, 0)}
         eeg_raw = {0: load_sensor("eeg", eeg, 0)}
-        fw_raw = {0: load_f_words(0)}
+        fw_first = load_f_words(0, 1)
         for q in range(4):
             nc.sync.dma_start(out=f_scales_raw[32 * q:32 * q + 4, :], in_=inv_eeg_scales[0, 4 * q:4 * q + 4, :].bitcast(I32))
         im_raw[1] = load_inv_meg(1)
-        fw_raw[1] = load_f_words(1)
+        fw_rest = load_f_words(1, GROUPS)
         im_raw[2] = load_inv_meg(2)
         meg_raw[1] = load_sensor("meg", meg, 1)
-        eeg_raw[1] = load_sensor("eeg", eeg, 1)
         im_raw[3] = load_inv_meg(3)
+        eeg_raw[1] = load_sensor("eeg", eeg, 1)
         ps_raw = load_parcel_vector("ps_raw", power_scale)
-        gain_cols = load_parcel_vector("gain_cols", gain)
+        gain_raw = load_parcel_vector("gain_raw", gain)
         pw_raw = [load_parcel_weights(g) for g in range(GROUPS)]
 
-        def interleave_inv_meg(g):
+        def interleave_inv_meg(g, copy):
             grouped = staging("inv_meg_grouped%d" % g)
-            nc.vector.tensor_copy(
+            copy(
                 out=grouped[:].rearrange("p (t m e j) -> p t m j e", t=4, e=4, j=4),
                 in_=im_raw[g][:].rearrange("p j (m t e) -> p t m j e", t=4, e=4))
             return grouped
 
-        def interleave_parcel_weights(g):
+        def interleave_parcel_weights(g, copy):
             grouped = staging("pw_grouped%d" % g)
-            nc.vector.tensor_copy(
+            copy(
                 out=grouped[:].rearrange("p (u m t) -> p m t u", u=4, t=4),
                 in_=pw_raw[g][:].rearrange("p t (m u) -> p m t u", u=4))
             return grouped
 
-        def interleave(name, slots, copy=nc.vector.tensor_copy):
+        def interleave_power(name, slots, copy):
             grouped = staging(name + "_grouped")
             copy(
-                out=grouped[:].rearrange("p (c i t) -> p c t i", i=4, t=4),
-                in_=slots[:].rearrange("p t (c i) -> p c t i", i=4))
+                out=grouped[:].rearrange("p (g c i t) -> p g c t i", g=slots.shape[1], i=4, t=4),
+                in_=slots.rearrange("p g t (c i) -> p g c t i", i=4))
             return grouped
 
         def transpose_sensor(name, raw, first_bank):
@@ -146,10 +146,10 @@ def tile_minimum_norm_parcel_power_k6_kernel(
         f_words = sbuf("f_words", [P, 4096], U8)
         f_scales = sbuf("f_scales", [P, 2048], U8)
 
-        def sort_f_words(gg):
+        def sort_f_words(raw, g0, g1):
             nc.vector.tensor_copy(
-                out=f_words[:, 2048 * gg:2048 * (gg + 1)].bitcast(I32).rearrange("p (g t m w) -> p g t m w", g=2, t=4, w=2),
-                in_=fw_raw[gg][:].rearrange("p (g m t w) -> p g t m w", g=2, t=4, w=2))
+                out=f_words[:, 1024 * g0:1024 * g1].bitcast(I32).rearrange("p (g t m w) -> p g t m w", t=4, m=32, w=2),
+                in_=raw[:].rearrange("p (g m t w) -> p g t m w", t=4, m=32, w=2))
 
         def meg_pass(h, g, t):
             cur = bank(4 + t, "j%d%d%d" % (h, g, t), [P, HALF], F32)
@@ -167,62 +167,73 @@ def tile_minimum_norm_parcel_power_k6_kernel(
                 rhs=eeg_q[h][0][:].bitcast(FP8X4), rhs_scale=eeg_q[h][1][:], start=False, stop=True)
 
         def square(h, g, t, cur):
-            nc.scalar.activation(out=d_slots[h, g][:, t, :], in_=cur[:], func=ACT.Square, scale=root_w[:, 4 * t + g:4 * t + g + 1])
+            nc.scalar.activation(
+                out=d_slots[h, g // 2][:, g % 2, t, :], in_=cur[:], func=ACT.Square,
+                scale=root_w[:, 4 * t + g:4 * t + g + 1])
 
         def currents(h, g):
-            d_slots[h, g] = sbuf("d_slots%d%d" % (h, g), [P, 4, HALF], BF16)
             for t in range(4):
                 cur = meg_pass(h, g, t)
                 eeg_pass(h, g, t, cur)
                 square(h, g, t, cur)
 
-        def parcels(h, g):
+        def parcel_pass(out, g, u, power):
             codes, scales = pw_q[g]
+            cols = slice(P * u, P * (u + 1))
+            nc.tensor.matmul_mx(
+                out=out, lhsT=codes[:, cols].bitcast(FP8X4), lhsT_scale=scales[:, cols],
+                rhs=power[0].bitcast(FP8X4), rhs_scale=power[1], start=(g == 0), stop=(g == GROUPS - 1))
+
+        def logarithm(tok, u, sums):
+            nc.scalar.activation(out=logs[tok.start][:, u, :], in_=sums, func=ACT.Ln, scale=ps_cols[:, u:u + 1], bias=1.0)
+
+        def gain_on_vector(tok, u):
+            nc.vector.tensor_scalar(out=y_slots[tok.start][:, u, :], in0=logs[tok.start][:, u, :], scalar1=gain_cols[:, u:u + 1], scalar2=None, op0=ALU.mult)
+
+        def gain_on_scalar(tok, u):
+            nc.scalar.activation(out=y_slots[tok.start][:, u, :], in_=logs[tok.start][:, u, :], func=ACT.Copy, scale=gain_cols[:, u:u + 1])
+
+        def transpose_y(tok, first_bank):
+            tiles = range(tok.start // P, tok.stop // P)
+            for n, i in enumerate(tiles):
+                y_banks[i] = bank(first_bank + n, "yt%d" % i, [P, 4, P], F32)
             for u in range(4):
-                if g == 0:
-                    r_banks[h, u] = bank(4 * h + u, "r%d%d" % (h, u), [P, HALF], F32)
-                cols = slice(P * u, P * (u + 1))
-                nc.tensor.matmul_mx(
-                    out=r_banks[h, u][:], lhsT=codes[:, cols].bitcast(FP8X4), lhsT_scale=scales[:, cols],
-                    rhs=d_q[h, g][0][:].bitcast(FP8X4), rhs_scale=d_q[h, g][1][:],
-                    start=(g == 0), stop=(g == GROUPS - 1))
+                for n, i in enumerate(tiles):
+                    nc.tensor.transpose(y_banks[i][:, u, :], y_slots[tok.start][:, u, P * n:P * (n + 1)], ident32[:])
 
-        def logarithm(h):
-            logs[h] = sbuf("logs%d" % h, [P, 4, HALF], F32)
-            for u in range(4):
-                nc.scalar.activation(out=logs[h][:, u, :], in_=r_banks[h, u][:], func=ACT.Ln, scale=ps_cols[:, u:u + 1], bias=1.0)
+        def store_y(i, copy):
+            rows = sb.tile([P, NP], F32, name="y_rows%d" % i, tag="y_rows", bufs=6, align_bytes=64)
+            copy(out=rows[:].rearrange("p (m u) -> p m u", u=4), in_=y_banks[i][:].rearrange("p u m -> p m u"))
+            nc.sync.dma_start(out=out_0[P * i:P * (i + 1), :], in_=rows[:])
 
-        def apply_gain(h):
-            y_slots[h] = sbuf("y_slots%d" % h, [P, 4, HALF], F32)
-            for u in range(4):
-                nc.vector.tensor_scalar(out=y_slots[h][:, u, :], in0=logs[h][:, u, :], scalar1=gain_cols[:, u:u + 1], scalar2=None, op0=ALU.mult)
+        def interleave_y(tok):
+            grouped = staging("y_grouped%d" % tok.start)
+            part = grouped[:, 0:4 * (tok.stop - tok.start)]
+            nc.vector.tensor_copy(
+                out=part.rearrange("p (c i u) -> p c u i", i=4, u=4),
+                in_=y_slots[tok.start][:].rearrange("p u (c i) -> p c u i", i=4))
+            return part
 
-        def transpose_y(h):
-            for i in range(4):
-                y_banks[h, i] = bank(i, "yt%d%d" % (h, i), [P, 4, P], F32)
-            for u in range(4):
-                for i in range(4):
-                    nc.tensor.transpose(y_banks[h, i][:, u, :], y_slots[h][:, u, P * i:P * (i + 1)], ident32[:])
+        def store_y_codes(tok, grouped):
+            nc.vector.quantize_mx(out=y_codes[:, tok].bitcast(FP8X4), scales=y_scales[:, tok], in_=grouped)
+            nc.sync.dma_start(out=out_1[0, :, tok, :].rearrange("p m t -> p (m t)").bitcast(I32), in_=y_codes[:, tok].bitcast(I32))
 
-        def store_y(h, i, on_vector):
-            rows = sbuf("y_rows%d%d" % (h, i), [P, NP], F32)
-            src = y_banks[h, i][:].rearrange("p u m -> p m u")
-            dst = rows[:].rearrange("p (m u) -> p m u", u=4)
-            if on_vector:
-                nc.vector.tensor_copy(out=dst, in_=src)
-            else:
-                nc.scalar.copy(out=dst, in_=src)
-            r0 = HALF * h + P * i
-            nc.sync.dma_start(out=out_0[r0:r0 + P, :], in_=rows[:])
-
-        def store_planes(h, codes, scales):
-            cols = slice(HALF * h, HALF * (h + 1))
-            nc.sync.dma_start(out=out_1[0, :, cols, :].rearrange("p m t -> p (m t)").bitcast(I32), in_=codes[:].bitcast(I32))
+        def store_y_scales(tok, queue):
             for q in range(4):
-                nc.sync.dma_start(out=out_2[0, 4 * q:4 * q + 4, cols].bitcast(I32), in_=scales[32 * q:32 * q + 4, :].bitcast(I32))
+                queue.dma_start(out=out_2[0, 4 * q:4 * q + 4, tok].bitcast(I32), in_=y_scales[32 * q:32 * q + 4, tok].bitcast(I32))
 
-        im_q, meg_q, eeg_q, pw_q, d_q = {}, {}, {}, {}, {}
-        d_slots, r_banks, logs, y_slots, y_banks = {}, {}, {}, {}, {}
+        im_q, meg_q, eeg_q, pw_q, d_q, y_banks = {}, {}, {}, {}, {}, {}
+        d_slots = {}
+        for h in range(2):
+            for gg in range(2):
+                d_slots[h, gg] = sbuf("d_slots%d%d" % (h, gg), [P, 2, 4, HALF], BF16)
+        logs, y_slots = {}, {}
+        for start, width in ((0, 512), (512, 256), (768, 256)):
+            logs[start] = sbuf("logs%d" % start, [P, 4, width], F32)
+            y_slots[start] = sbuf("y_slots%d" % start, [P, 4, width], F32)
+        y_codes = sbuf("y_codes", [P, T], U32)
+        y_scales = sbuf("y_scales", [P, T], U8)
+        on_vector, on_scalar = nc.vector.tensor_copy, nc.scalar.copy
 
         nc.vector.tensor_copy(
             out=w_rows[0:GROUPS, :].rearrange("g (t m e) -> g t m e", t=4, e=4),
@@ -234,99 +245,127 @@ def tile_minimum_norm_parcel_power_k6_kernel(
         w_cols = sbuf("w_cols", [P, 4, GROUPS], F32)
         nc.scalar.activation(out=root0[:], in_=w_turned[:, :, 0:GROUPS], func=ACT.Sqrt)
         nc.scalar.copy(out=w_cols[:], in_=w_turned[:, :, 0:GROUPS])
+        ln_warm = sbuf("ln_warm", [P, 16], F32)
+        nc.scalar.activation(out=ln_warm[:], in_=w_cols[:].rearrange("p t g -> p (t g)"), func=ACT.Ln)
+        grouped = interleave_inv_meg(0, on_vector)
         inv_root = sbuf("inv_root", [P, 16], F32)
         nc.vector.reciprocal(out=inv_root[:], in_=root0[:].rearrange("p t g -> p (t g)"))
 
         meg_grouped = gather_sensor("meg0", transpose_sensor("meg0", meg_raw[0], 0))
         eeg_grouped = gather_sensor("eeg0", transpose_sensor("eeg0", eeg_raw[0], 2))
-        grouped = interleave_inv_meg(0)
+        im_q[0] = quantize("inv_meg0", grouped)
         half_quot = sbuf("half_quot", [P, 16], F32)
         nc.vector.scalar_tensor_tensor(
             out=half_quot[:], in0=w_cols[:].rearrange("p t g -> p (t g)"), scalar=0.5, in1=inv_root[:], op0=ALU.mult, op1=ALU.mult)
-        im_q[0] = quantize("inv_meg0", grouped)
-        meg_q[0] = quantize("meg0", meg_grouped)
-        root_w = sbuf("root_w", [P, 16], F32)
-        nc.vector.scalar_tensor_tensor(
-            out=root_w[:], in0=root0[:].rearrange("p t g -> p (t g)"), scalar=0.5, in1=half_quot[:], op0=ALU.mult, op1=ALU.add)
-        sort_f_words(0)
         nc.vector.tensor_copy(
             out=f_scales[:].bitcast(I32).rearrange("p (g t m) -> p g t m", g=GROUPS, t=4),
             in_=f_scales_raw[:].rearrange("p (g m t) -> p g t m", g=GROUPS, t=4))
+        root_w = sbuf("root_w", [P, 16], F32)
+        nc.vector.scalar_tensor_tensor(
+            out=root_w[:], in0=root0[:].rearrange("p t g -> p (t g)"), scalar=0.5, in1=half_quot[:], op0=ALU.mult, op1=ALU.add)
+        meg_q[0] = quantize("meg0", meg_grouped)
+        sort_f_words(fw_first, 0, 1)
         eeg_q[0] = quantize("eeg0", eeg_grouped)
 
-        d_slots[0, 0] = sbuf("d_slots00", [P, 4, HALF], BF16)
         first = [meg_pass(0, 0, t) for t in range(4)]
         for t in range(4):
             eeg_pass(0, 0, t, first[t])
             square(0, 0, t, first[t])
 
-        grouped = interleave_inv_meg(1)
-        sort_f_words(1)
-        im_q[1] = quantize("inv_meg1", grouped)
+        def power(h, g, copy):
+            return interleave_power("d%d%d" % (h, g), d_slots[h, g // 2][:, g % 2:g % 2 + 1], copy)
+
+        def quarter(c, gg, copy):
+            return interleave_power("dq%d%d" % (c, gg), d_slots[1, gg][:, :, :, 256 * c:256 * (c + 1)], copy)
+
+        a = interleave_inv_meg(1, on_vector)
+        sort_f_words(fw_rest, 1, GROUPS)
+        im_q[1] = quantize("inv_meg1", a)
         currents(0, 1)
-
-        grouped = interleave_inv_meg(2)
-        d_grouped = interleave("d00", d_slots[0, 0])
-        im_q[2] = quantize("inv_meg2", grouped)
-        d_q[0, 0] = quantize("d00", d_grouped)
+        a = interleave_inv_meg(2, on_vector)
+        b = power(0, 0, on_vector)
+        im_q[2] = quantize("inv_meg2", a)
         meg_grouped = gather_sensor("meg1", transpose_sensor("meg1", meg_raw[1], 0))
-        eeg_grouped = gather_sensor("eeg1", transpose_sensor("eeg1", eeg_raw[1], 2))
         currents(0, 2)
-
-        grouped = interleave_inv_meg(3)
-        meg_q[1] = quantize("meg1", meg_grouped)
-        im_q[3] = quantize("inv_meg3", grouped)
-        eeg_q[1] = quantize("eeg1", eeg_grouped)
-        ps_cols = sbuf("ps_cols", [P, 4], F32)
-        nc.scalar.copy(out=ps_cols[:], in_=ps_raw[:])
+        a = interleave_inv_meg(3, on_vector)
+        d_q[0] = quantize("d00", b)
+        im_q[3] = quantize("inv_meg3", a)
+        eeg_grouped = gather_sensor("eeg1", transpose_sensor("eeg1", eeg_raw[1], 2))
         currents(0, 3)
 
-        def prepare(pw_g, d_hg):
-            a = interleave_parcel_weights(pw_g)
-            b = interleave("d%d%d" % d_hg, d_slots[d_hg])
-            pw_q[pw_g] = quantize("pw%d" % pw_g, a)
-            d_q[d_hg] = quantize("d%d%d" % d_hg, b)
+        b = power(0, 1, on_vector)
+        meg_q[1] = quantize("meg1", meg_grouped)
+        d_q[1] = quantize("d01", b)
+        eeg_q[1] = quantize("eeg1", eeg_grouped)
+        ps_cols = sbuf("ps_cols", [P, 4], F32)
+        gain_cols = sbuf("gain_cols", [P, 4], F32)
+        nc.scalar.copy(out=ps_cols[:], in_=ps_raw[:])
+        nc.scalar.copy(out=gain_cols[:], in_=gain_raw[:])
+        for g in range(GROUPS):
+            currents(1, g)
 
-        prepare(0, (0, 1))
-        currents(1, 0)
-        prepare(1, (0, 2))
-        currents(1, 1)
-        parcels(0, 0)
-        prepare(2, (0, 3))
-        currents(1, 2)
-        parcels(0, 1)
-        prepare(3, (1, 0))
-        currents(1, 3)
-        last = interleave("d13", d_slots[1, 3], nc.scalar.copy)
-        parcels(0, 2)
-        parcels(0, 3)
-        logarithm(0)
+        for g in range(2):
+            a = interleave_parcel_weights(g, on_vector)
+            b = power(0, g + 2, on_vector)
+            pw_q[g] = quantize("pw%d" % g, a)
+            d_q[g + 2] = quantize("d0%d" % (g + 2), b)
+        a = interleave_parcel_weights(2, on_vector)
+        b = interleave_parcel_weights(3, on_vector)
+        pw_q[2] = quantize("pw2", a)
+        a = quarter(0, 0, on_vector)
+        pw_q[3] = quantize("pw3", b)
+        qa0 = quantize("dq00", a)
+        late_a = quarter(0, 1, on_scalar)
 
-        a = interleave("d11", d_slots[1, 1])
-        b = interleave("d12", d_slots[1, 2])
-        d_q[1, 1] = quantize("d11", a)
-        parcels(1, 0)
-        parcels(1, 1)
-        apply_gain(0)
-        d_q[1, 2] = quantize("d12", b)
-        d_q[1, 3] = quantize("d13", last)
-        parcels(1, 2)
-        transpose_y(0)
-        parcels(1, 3)
-        y_grouped = interleave("y0", y_slots[0])
-        for i in range(2):
-            store_y(0, i, False)
-        logarithm(1)
-        store_y(0, 2, True)
-        y_q = quantize("y0", y_grouped)
-        store_y(0, 3, False)
-        store_planes(0, *y_q)
-        apply_gain(1)
-        transpose_y(1)
-        y_grouped = interleave("y1", y_slots[1])
-        store_y(1, 0, False)
-        store_y(1, 1, False)
-        y_q = quantize("y1", y_grouped)
-        store_y(1, 2, False)
-        store_planes(1, *y_q)
-        store_y(1, 3, True)
+        half0, tok_a, tok_b = slice(0, 512), slice(512, 768), slice(768, 1024)
+        sums = [bank(u, "r0%d" % u, [P, HALF], F32) for u in range(4)]
+        for g in range(GROUPS):
+            for u in range(4):
+                parcel_pass(sums[u][:], g, u, d_q[g])
+        for u in range(4):
+            logarithm(half0, u, sums[u][:])
+        a = quarter(1, 0, on_vector)
+        qa1 = quantize("dq01", late_a)
+        b = quarter(1, 1, on_vector)
+        for u in range(4):
+            gain_on_vector(half0, u)
+        qb0 = quantize("dq10", a)
+        qb1 = quantize("dq11", b)
+
+        def columns(pair, g):
+            cols = slice(256 * (g % 2), 256 * (g % 2 + 1))
+            return pair[g // 2][0][:, cols], pair[g // 2][1][:, cols]
+
+        sums_a = [bank(4 + n, "ra%d" % n, [P, 2, 256], F32) for n in range(2)]
+        for u in range(4):
+            for g in range(GROUPS):
+                parcel_pass(sums_a[u // 2][:, u % 2, :], g, u, columns((qa0, qa1), g))
+        transpose_y(half0, 0)
+        for u in range(4):
+            logarithm(tok_a, u, sums_a[u // 2][:, u % 2, :])
+        sums_b = [bank(6 + n, "rb%d" % n, [P, 2, 256], F32) for n in range(2)]
+        for u in range(4):
+            for g in range(GROUPS):
+                parcel_pass(sums_b[u // 2][:, u % 2, :], g, u, columns((qb0, qb1), g))
+        for u in range(4):
+            gain_on_vector(tok_a, u)
+        y_grouped = interleave_y(half0)
+        for i in range(3):
+            store_y(i, on_scalar)
+        transpose_y(tok_a, 4)
+        for u in range(4):
+            logarithm(tok_b, u, sums_b[u // 2][:, u % 2, :])
+        y_grouped_a = interleave_y(tok_a)
+        store_y_codes(half0, y_grouped)
+        store_y(3, on_scalar)
+        for u in range(4):
+            gain_on_vector(tok_b, u)
+        for i in range(4, 6):
+            store_y(i, on_scalar)
+        store_y_codes(tok_a, y_grouped_a)
+        transpose_y(tok_b, 6)
+        y_grouped = interleave_y(tok_b)
+        store_y(6, on_scalar)
+        store_y_codes(tok_b, y_grouped)
+        store_y(7, on_vector)
+        store_y_scales(slice(0, T), nc.sync)

@@ -3,8 +3,8 @@ from contextlib import ExitStack
 import concourse.mybir as mybir
 from concourse.masks import make_identity
 
-T, C, S, NP = 1024, 512, 2048, 512
-FLOPS = 2 * T * (2 * C * S + S * NP)
+SAMPLES, CHANNELS, SOURCES, PARCELS = 1024, 512, 2048, 512
+FLOPS = 2 * SAMPLES * (2 * CHANNELS * SOURCES + SOURCES * PARCELS)
 
 F32 = mybir.dt.float32
 BF16 = mybir.dt.bfloat16
@@ -17,8 +17,13 @@ ACT = mybir.ActivationFunctionType
 ALU = mybir.AluOpType
 
 P = 128
+SLOTS = 4
+K_PASS = P * SLOTS
+GROUPS = SOURCES // K_PASS
 HALF = 512
-GROUPS = S // 512
+QUARTER = 256
+STAGING_BUFS = 5
+ROW_BUFS = 6
 
 
 def tile_minimum_norm_parcel_power_k6_kernel(
@@ -30,25 +35,20 @@ def tile_minimum_norm_parcel_power_k6_kernel(
         sb = ctx.enter_context(tc.tile_pool(name="sb", bufs=1))
         ps = ctx.enter_context(tc.psum_pool(name="ps", bufs=1))
         ctx.enter_context(tc.manual_schedule())
+        on_vector, on_scalar = nc.vector.tensor_copy, nc.scalar.copy
 
         def sbuf(name, shape, dtype):
             return sb.tile(shape, dtype, name=name, align_bytes=64)
 
         def staging(name):
-            return sb.tile([P, 2048], BF16, name=name, tag="grouped", bufs=5, align_bytes=64)
+            return sb.tile([P, SLOTS * K_PASS], BF16, name=name, tag="staging", bufs=STAGING_BUFS, align_bytes=64)
 
-        def bank(b, name, shape, dtype):
-            return ps.tile(shape, dtype, name=name, tag="bank%d" % b)
+        def bank(number, name, shape, dtype):
+            return ps.tile(shape, dtype, name=name, tag="bank%d" % number)
 
-        def quantize(name, grouped):
-            codes = sbuf(name + "_codes", [P, 512], U32)
-            scales = sbuf(name + "_scales", [P, 512], U8)
-            nc.vector.quantize_mx(out=codes[:].bitcast(FP8X4), scales=scales[:], in_=grouped[:])
-            return codes[:], scales[:]
-
-        w_rows = sbuf("w_rows", [P, 512], BF16)
+        w_rows = sbuf("w_rows", [P, K_PASS], BF16)
         nc.vector.memset(w_rows[:], 0.0)
-        f_scales_raw = sbuf("f_scales_raw", [P, 512], I32)
+        f_scales_raw = sbuf("f_scales_raw", [P, SOURCES // 4], I32)
         nc.vector.memset(f_scales_raw[:], 0)
         ident16 = sbuf("ident16", [P, P], BF16)
         make_identity(nc, ident16[:])
@@ -56,316 +56,333 @@ def tile_minimum_norm_parcel_power_k6_kernel(
         make_identity(nc, ident32[:])
 
         def load_inv_meg(g):
-            raw = sbuf("inv_meg_raw%d" % g, [P, 4, 512], BF16)
-            nc.sync.dma_start(out=raw[:], in_=inv_meg[:, 512 * g:512 * (g + 1)].rearrange("(p j) n -> p j n", j=4))
+            raw = sbuf("inv_meg_raw%d" % g, [P, SLOTS, K_PASS], BF16)
+            cols = inv_meg[:, K_PASS * g:K_PASS * (g + 1)]
+            nc.sync.dma_start(out=raw[:], in_=cols.rearrange("(p j) n -> p j n", j=SLOTS))
             return raw
 
-        def load_sensor(name, x, h):
-            raws = []
-            for a in range(2):
-                raw = sbuf("%s_raw%d%d" % (name, h, a), [P, 2 * C], BF16)
-                r0 = HALF * h + 256 * a
-                nc.sync.dma_start(out=raw[:], in_=x[r0:r0 + 256, :].rearrange("(p i) k -> p (i k)", i=2))
-                raws.append(raw)
-            return raws
+        def load_sensor_quarters(name, x):
+            quarters = []
+            for c in range(2):
+                raw = sbuf("%s_raw0%d" % (name, c), [P, 2 * CHANNELS], BF16)
+                rows = x[QUARTER * c:QUARTER * (c + 1), :]
+                nc.sync.dma_start(out=raw[:], in_=rows.rearrange("(p i) k -> p (i k)", i=2))
+                quarters.append(raw[:])
+            return quarters
+
+        def load_sensor_half(name, x):
+            raw = sbuf("%s_raw1" % name, [P, 4 * CHANNELS], BF16)
+            nc.sync.dma_start(
+                out=raw[:].rearrange("p (c k) -> p c k", c=2),
+                in_=x[HALF:, :].rearrange("(c p i) k -> p c (i k)", c=2, i=2))
+            return [raw[:, 2 * CHANNELS * c:2 * CHANNELS * (c + 1)] for c in range(2)]
 
         def load_f_words(g0, g1):
-            raw = sbuf("f_words_raw%d" % g0, [P, 256 * (g1 - g0)], I32)
-            nc.sync.dma_start(out=raw[:], in_=inv_eeg_words[0, :, 1024 * g0:1024 * g1].bitcast(I32))
+            raw = sbuf("f_words_raw%d" % g0, [P, K_PASS // 2 * (g1 - g0)], I32)
+            nc.sync.dma_start(out=raw[:], in_=inv_eeg_words[0, :, 2 * K_PASS * g0:2 * K_PASS * g1].bitcast(I32))
             return raw
 
         def load_parcel_weights(g):
-            raw = sbuf("pw_raw%d" % g, [P, 4, NP], BF16)
-            rows = parcel_weights[512 * g:512 * (g + 1), :].rearrange("(m t e) n -> t m e n", t=4, e=4)
-            for t in range(4):
+            raw = sbuf("pw_raw%d" % g, [P, SLOTS, PARCELS], BF16)
+            rows = parcel_weights[K_PASS * g:K_PASS * (g + 1), :].rearrange("(m t e) n -> t m e n", t=SLOTS, e=4)
+            for t in range(SLOTS):
                 nc.sync.dma_start(out=raw[:, t, :], in_=rows[t])
             return raw
 
         def load_parcel_vector(name, vec):
-            raw = sbuf(name, [P, 4], BF16)
-            nc.sync.dma_start(out=raw[:], in_=vec.rearrange("(p u) -> p u", u=4))
+            raw = sbuf(name, [P, SLOTS], BF16)
+            nc.sync.dma_start(out=raw[:], in_=vec.rearrange("(p u) -> p u", u=SLOTS))
             return raw
 
-        w_raw = sbuf("w_raw", [GROUPS, 512], BF16)
+        inv_meg_raw, meg_raw, eeg_raw = {}, {}, {}
+        w_raw = sbuf("w_raw", [GROUPS, K_PASS], BF16)
         nc.sync.dma_start(out=w_raw[:], in_=source_weight.rearrange("(g s) -> g s", g=GROUPS))
-        im_raw = {0: load_inv_meg(0)}
-        meg_raw = {0: load_sensor("meg", meg, 0)}
-        eeg_raw = {0: load_sensor("eeg", eeg, 0)}
-        fw_first = load_f_words(0, 1)
-        for q in range(4):
-            nc.sync.dma_start(out=f_scales_raw[32 * q:32 * q + 4, :], in_=inv_eeg_scales[0, 4 * q:4 * q + 4, :].bitcast(I32))
-        im_raw[1] = load_inv_meg(1)
-        fw_rest = load_f_words(1, GROUPS)
-        im_raw[2] = load_inv_meg(2)
-        meg_raw[1] = load_sensor("meg", meg, 1)
-        im_raw[3] = load_inv_meg(3)
-        eeg_raw[1] = load_sensor("eeg", eeg, 1)
-        ps_raw = load_parcel_vector("ps_raw", power_scale)
+        inv_meg_raw[0] = load_inv_meg(0)
+        meg_raw[0] = load_sensor_quarters("meg", meg)
+        eeg_raw[0] = load_sensor_quarters("eeg", eeg)
+        f_words_first = load_f_words(0, 1)
+        for quad in range(4):
+            nc.sync.dma_start(
+                out=f_scales_raw[32 * quad:32 * quad + 4, :],
+                in_=inv_eeg_scales[0, 4 * quad:4 * quad + 4, :].bitcast(I32))
+        inv_meg_raw[1] = load_inv_meg(1)
+        f_words_rest = load_f_words(1, GROUPS)
+        inv_meg_raw[2] = load_inv_meg(2)
+        meg_raw[1] = load_sensor_half("meg", meg)
+        inv_meg_raw[3] = load_inv_meg(3)
+        eeg_raw[1] = load_sensor_half("eeg", eeg)
+        power_scale_raw = load_parcel_vector("power_scale_raw", power_scale)
         gain_raw = load_parcel_vector("gain_raw", gain)
         pw_raw = [load_parcel_weights(g) for g in range(GROUPS)]
 
-        def interleave_inv_meg(g, copy):
+        def quantize(name, grouped):
+            codes = sbuf(name + "_codes", [P, K_PASS], U32)
+            scales = sbuf(name + "_scales", [P, K_PASS], U8)
+            nc.vector.quantize_mx(out=codes[:].bitcast(FP8X4), scales=scales[:], in_=grouped[:])
+            return codes[:], scales[:]
+
+        def interleave_inv_meg(g):
             grouped = staging("inv_meg_grouped%d" % g)
-            copy(
-                out=grouped[:].rearrange("p (t m e j) -> p t m j e", t=4, e=4, j=4),
-                in_=im_raw[g][:].rearrange("p j (m t e) -> p t m j e", t=4, e=4))
+            nc.vector.tensor_copy(
+                out=grouped[:].rearrange("p (t m e j) -> p m t j e", t=SLOTS, e=4, j=SLOTS),
+                in_=inv_meg_raw[g][:].rearrange("p j (m t e) -> p m t j e", t=SLOTS, e=4))
             return grouped
 
-        def interleave_parcel_weights(g, copy):
+        def interleave_parcel_weights(g):
             grouped = staging("pw_grouped%d" % g)
-            copy(
-                out=grouped[:].rearrange("p (u m t) -> p m t u", u=4, t=4),
-                in_=pw_raw[g][:].rearrange("p t (m u) -> p m t u", u=4))
+            nc.vector.tensor_copy(
+                out=grouped[:].rearrange("p (u n t) -> p n t u", u=SLOTS, t=SLOTS),
+                in_=pw_raw[g][:].rearrange("p t (n u) -> p n t u", u=SLOTS))
             return grouped
 
         def interleave_power(name, slots, copy):
             grouped = staging(name + "_grouped")
             copy(
-                out=grouped[:].rearrange("p (g c i t) -> p g c t i", g=slots.shape[1], i=4, t=4),
-                in_=slots.rearrange("p g t (c i) -> p g c t i", i=4))
+                out=grouped[:].rearrange("p (g r i t) -> p g r t i", g=slots.shape[1], i=4, t=SLOTS),
+                in_=slots.rearrange("p g t (r i) -> p g r t i", i=4))
             return grouped
 
-        def transpose_sensor(name, raw, first_bank):
-            banks = []
-            for a in range(2):
-                turned = bank(first_bank + a, "%s_turned%d" % (name, a), [P, 2, 2, P], F32)
+        def turn_sensor(name, quarters, first_bank):
+            turned = []
+            for c in range(2):
+                both = bank(first_bank + c, "%s_turned%d" % (name, c), [P, 2, 2, P], F32)
+                words = quarters[c].bitcast(F32)
                 for i in range(2):
-                    words = raw[a][:].bitcast(F32)
-                    for u in range(2):
-                        nc.tensor.transpose(turned[:, i, u, :], words[:, 256 * i + u:256 * (i + 1):2], ident32[:])
-                banks.append(turned)
-            return banks
-
-        def gather_sensor(name, banks):
-            grouped = sbuf(name + "_grouped", [P, 2048], BF16)
-            words = grouped[:].bitcast(F32).rearrange("p (a r i u) -> p a r i u", a=2, i=2, u=2)
-            for a in range(2):
-                nc.scalar.copy(out=words[:, a], in_=banks[a][:].rearrange("p i u r -> p r i u"))
+                    for w in range(2):
+                        row_words = words[:, CHANNELS // 2 * i + w:CHANNELS // 2 * (i + 1):2]
+                        nc.tensor.transpose(both[:, i, w, :], row_words, ident32[:])
+                turned.append(both)
+            grouped = sbuf(name + "_grouped", [P, SLOTS * HALF], BF16)
+            grouped_words = grouped[:].bitcast(F32).rearrange("p (c r i w) -> p c r i w", c=2, i=2, w=2)
+            for c in range(2):
+                nc.scalar.copy(out=grouped_words[:, c], in_=turned[c][:].rearrange("p i w r -> p r i w"))
             return grouped
 
-        f_words = sbuf("f_words", [P, 4096], U8)
-        f_scales = sbuf("f_scales", [P, 2048], U8)
+        f_words = sbuf("f_words", [P, 2 * SOURCES], U8)
+        f_scales = sbuf("f_scales", [P, SOURCES], U8)
 
         def sort_f_words(raw, g0, g1):
+            sorted_words = f_words[:, 2 * K_PASS * g0:2 * K_PASS * g1].bitcast(I32)
             nc.vector.tensor_copy(
-                out=f_words[:, 1024 * g0:1024 * g1].bitcast(I32).rearrange("p (g t m w) -> p g t m w", t=4, m=32, w=2),
-                in_=raw[:].rearrange("p (g m t w) -> p g t m w", t=4, m=32, w=2))
+                out=sorted_words.rearrange("p (g t m x) -> p g m t x", t=SLOTS, m=32, x=2),
+                in_=raw.rearrange("p (g m t x) -> p g m t x", t=SLOTS, m=32, x=2))
+
+        inv_meg_q, meg_q, eeg_q = {}, {}, {}
+        d_slots = {}
+        for h in range(2):
+            for pair in range(GROUPS // 2):
+                d_slots[h, pair] = sbuf("d_slots%d%d" % (h, pair), [P, 2, SLOTS, HALF], BF16)
 
         def meg_pass(h, g, t):
-            cur = bank(4 + t, "j%d%d%d" % (h, g, t), [P, HALF], F32)
-            codes, scales = im_q[g]
+            current = bank(4 + t, "j%d%d%d" % (h, g, t), [P, HALF], F32)
+            codes, scales = inv_meg_q[g]
             cols = slice(P * t, P * (t + 1))
             nc.tensor.matmul_mx(
-                out=cur[:], lhsT=codes[:, cols].bitcast(FP8X4), lhsT_scale=scales[:, cols],
-                rhs=meg_q[h][0][:].bitcast(FP8X4), rhs_scale=meg_q[h][1][:], start=True, stop=False)
-            return cur
+                out=current[:], lhsT=codes[:, cols].bitcast(FP8X4), lhsT_scale=scales[:, cols],
+                rhs=meg_q[h][0].bitcast(FP8X4), rhs_scale=meg_q[h][1], start=True, stop=False)
+            return current
 
-        def eeg_pass(h, g, t, cur):
-            c0 = 512 * g + P * t
+        def eeg_pass_and_square(h, g, t, current):
+            c0 = K_PASS * g + P * t
             nc.tensor.matmul_mx(
-                out=cur[:], lhsT=f_words[:, 2 * c0:2 * (c0 + P)].bitcast(FP4X4), lhsT_scale=f_scales[:, c0:c0 + P],
-                rhs=eeg_q[h][0][:].bitcast(FP8X4), rhs_scale=eeg_q[h][1][:], start=False, stop=True)
-
-        def square(h, g, t, cur):
+                out=current[:], lhsT=f_words[:, 2 * c0:2 * (c0 + P)].bitcast(FP4X4), lhsT_scale=f_scales[:, c0:c0 + P],
+                rhs=eeg_q[h][0].bitcast(FP8X4), rhs_scale=eeg_q[h][1], start=False, stop=True)
             nc.scalar.activation(
-                out=d_slots[h, g // 2][:, g % 2, t, :], in_=cur[:], func=ACT.Square,
-                scale=root_w[:, 4 * t + g:4 * t + g + 1])
+                out=d_slots[h, g // 2][:, g % 2, t, :], in_=current[:], func=ACT.Square,
+                scale=root_w[:, GROUPS * t + g:GROUPS * t + g + 1])
 
         def currents(h, g):
-            for t in range(4):
-                cur = meg_pass(h, g, t)
-                eeg_pass(h, g, t, cur)
-                square(h, g, t, cur)
+            for t in range(SLOTS):
+                eeg_pass_and_square(h, g, t, meg_pass(h, g, t))
 
-        def parcel_pass(out, g, u, power):
+        def first_half_power(g):
+            return interleave_power("d0%d" % g, d_slots[0, g // 2][:, g % 2:g % 2 + 1], on_vector)
+
+        def quarter_power(c, pair, copy):
+            slots = d_slots[1, pair][:, :, :, QUARTER * c:QUARTER * (c + 1)]
+            return interleave_power("dq%d%d" % (c, pair), slots, copy)
+
+        pw_q, d_q, y_banks, logs, y_slots = {}, {}, {}, {}, {}
+        first_half = slice(0, HALF)
+        third_quarter = slice(HALF, HALF + QUARTER)
+        last_quarter = slice(HALF + QUARTER, SAMPLES)
+        for span in (first_half, third_quarter, last_quarter):
+            logs[span.start] = sbuf("logs%d" % span.start, [P, SLOTS, span.stop - span.start], F32)
+            y_slots[span.start] = sbuf("y_slots%d" % span.start, [P, SLOTS, span.stop - span.start], F32)
+        y_codes = sbuf("y_codes", [P, SAMPLES], U32)
+        y_scales = sbuf("y_scales", [P, SAMPLES], U8)
+
+        def parcel_pass(out, g, u, power_codes, power_scales):
             codes, scales = pw_q[g]
             cols = slice(P * u, P * (u + 1))
             nc.tensor.matmul_mx(
                 out=out, lhsT=codes[:, cols].bitcast(FP8X4), lhsT_scale=scales[:, cols],
-                rhs=power[0].bitcast(FP8X4), rhs_scale=power[1], start=(g == 0), stop=(g == GROUPS - 1))
+                rhs=power_codes.bitcast(FP8X4), rhs_scale=power_scales, start=(g == 0), stop=(g == GROUPS - 1))
 
-        def logarithm(tok, u, sums):
-            nc.scalar.activation(out=logs[tok.start][:, u, :], in_=sums, func=ACT.Ln, scale=ps_cols[:, u:u + 1], bias=1.0)
+        def quarter_passes(first_bank, pairs):
+            banks = [bank(first_bank + n, "rq%d" % (first_bank + n), [P, 2, QUARTER], F32) for n in range(2)]
+            sums = [banks[u // 2][:, u % 2, :] for u in range(SLOTS)]
+            for u in range(SLOTS):
+                for g in range(GROUPS):
+                    codes, scales = pairs[g // 2]
+                    cols = slice(QUARTER * (g % 2), QUARTER * (g % 2 + 1))
+                    parcel_pass(sums[u], g, u, codes[:, cols], scales[:, cols])
+            return sums
 
-        def gain_on_vector(tok, u):
-            nc.vector.tensor_scalar(out=y_slots[tok.start][:, u, :], in0=logs[tok.start][:, u, :], scalar1=gain_cols[:, u:u + 1], scalar2=None, op0=ALU.mult)
+        def logarithm(span, sums, parcel_slots):
+            for u in parcel_slots:
+                nc.scalar.activation(
+                    out=logs[span.start][:, u, :], in_=sums[u], func=ACT.Ln,
+                    scale=power_scale_cols[:, u:u + 1], bias=1.0)
 
-        def gain_on_scalar(tok, u):
-            nc.scalar.activation(out=y_slots[tok.start][:, u, :], in_=logs[tok.start][:, u, :], func=ACT.Copy, scale=gain_cols[:, u:u + 1])
+        def apply_gain(span):
+            for u in range(SLOTS):
+                nc.vector.tensor_scalar(
+                    out=y_slots[span.start][:, u, :], in0=logs[span.start][:, u, :],
+                    scalar1=gain_cols[:, u:u + 1], scalar2=None, op0=ALU.mult)
 
-        def transpose_y(tok, first_bank):
-            tiles = range(tok.start // P, tok.stop // P)
+        def transpose_y(span, first_bank):
+            tiles = range(span.start // P, span.stop // P)
             for n, i in enumerate(tiles):
-                y_banks[i] = bank(first_bank + n, "yt%d" % i, [P, 4, P], F32)
-            for u in range(4):
+                y_banks[i] = bank(first_bank + n, "yt%d" % i, [P, SLOTS, P], F32)
+            for u in range(SLOTS):
                 for n, i in enumerate(tiles):
-                    nc.tensor.transpose(y_banks[i][:, u, :], y_slots[tok.start][:, u, P * n:P * (n + 1)], ident32[:])
+                    nc.tensor.transpose(y_banks[i][:, u, :], y_slots[span.start][:, u, P * n:P * (n + 1)], ident32[:])
 
         def store_y(i, copy):
-            rows = sb.tile([P, NP], F32, name="y_rows%d" % i, tag="y_rows", bufs=6, align_bytes=64)
-            copy(out=rows[:].rearrange("p (m u) -> p m u", u=4), in_=y_banks[i][:].rearrange("p u m -> p m u"))
+            rows = sb.tile([P, PARCELS], F32, name="y_rows%d" % i, tag="y_rows", bufs=ROW_BUFS, align_bytes=64)
+            copy(out=rows[:].rearrange("p (n u) -> p n u", u=SLOTS), in_=y_banks[i][:].rearrange("p u n -> p n u"))
             nc.sync.dma_start(out=out_0[P * i:P * (i + 1), :], in_=rows[:])
 
-        def interleave_y(tok):
-            grouped = staging("y_grouped%d" % tok.start)
-            part = grouped[:, 0:4 * (tok.stop - tok.start)]
+        def interleave_y(span):
+            grouped = staging("y_grouped%d" % span.start)
+            part = grouped[:, 0:SLOTS * (span.stop - span.start)]
             nc.vector.tensor_copy(
-                out=part.rearrange("p (c i u) -> p c u i", i=4, u=4),
-                in_=y_slots[tok.start][:].rearrange("p u (c i) -> p c u i", i=4))
+                out=part.rearrange("p (r i u) -> p r u i", i=4, u=SLOTS),
+                in_=y_slots[span.start][:].rearrange("p u (r i) -> p r u i", i=4))
             return part
 
-        def store_y_codes(tok, grouped):
-            nc.vector.quantize_mx(out=y_codes[:, tok].bitcast(FP8X4), scales=y_scales[:, tok], in_=grouped)
-            nc.sync.dma_start(out=out_1[0, :, tok, :].rearrange("p m t -> p (m t)").bitcast(I32), in_=y_codes[:, tok].bitcast(I32))
+        def quantize_y(span, grouped):
+            nc.vector.quantize_mx(out=y_codes[:, span].bitcast(FP8X4), scales=y_scales[:, span], in_=grouped)
 
-        def store_y_scales(tok, queue):
-            for q in range(4):
-                queue.dma_start(out=out_2[0, 4 * q:4 * q + 4, tok].bitcast(I32), in_=y_scales[32 * q:32 * q + 4, tok].bitcast(I32))
-
-        im_q, meg_q, eeg_q, pw_q, d_q, y_banks = {}, {}, {}, {}, {}, {}
-        d_slots = {}
-        for h in range(2):
-            for gg in range(2):
-                d_slots[h, gg] = sbuf("d_slots%d%d" % (h, gg), [P, 2, 4, HALF], BF16)
-        logs, y_slots = {}, {}
-        for start, width in ((0, 512), (512, 256), (768, 256)):
-            logs[start] = sbuf("logs%d" % start, [P, 4, width], F32)
-            y_slots[start] = sbuf("y_slots%d" % start, [P, 4, width], F32)
-        y_codes = sbuf("y_codes", [P, T], U32)
-        y_scales = sbuf("y_scales", [P, T], U8)
-        on_vector, on_scalar = nc.vector.tensor_copy, nc.scalar.copy
+        def store_y_codes(span):
+            nc.sync.dma_start(
+                out=out_1[0, :, span, :].rearrange("p n u -> p (n u)").bitcast(I32), in_=y_codes[:, span].bitcast(I32))
 
         nc.vector.tensor_copy(
-            out=w_rows[0:GROUPS, :].rearrange("g (t m e) -> g t m e", t=4, e=4),
-            in_=w_raw[:].rearrange("g (m t e) -> g t m e", t=4, e=4))
-        w_turned = bank(7, "w_turned", [P, 4, P], BF16)
-        for t in range(4):
+            out=w_rows[0:GROUPS, :].rearrange("g (t m e) -> g m t e", t=SLOTS, e=4),
+            in_=w_raw[:].rearrange("g (m t e) -> g m t e", t=SLOTS, e=4))
+        w_turned = bank(7, "w_turned", [P, SLOTS, P], BF16)
+        for t in range(SLOTS):
             nc.tensor.transpose(w_turned[:, t, :], w_rows[:, P * t:P * (t + 1)], ident16[:])
-        root0 = sbuf("root0", [P, 4, GROUPS], F32)
-        w_cols = sbuf("w_cols", [P, 4, GROUPS], F32)
-        nc.scalar.activation(out=root0[:], in_=w_turned[:, :, 0:GROUPS], func=ACT.Sqrt)
-        nc.scalar.copy(out=w_cols[:], in_=w_turned[:, :, 0:GROUPS])
-        ln_warm = sbuf("ln_warm", [P, 16], F32)
-        nc.scalar.activation(out=ln_warm[:], in_=w_cols[:].rearrange("p t g -> p (t g)"), func=ACT.Ln)
-        grouped = interleave_inv_meg(0, on_vector)
-        inv_root = sbuf("inv_root", [P, 16], F32)
-        nc.vector.reciprocal(out=inv_root[:], in_=root0[:].rearrange("p t g -> p (t g)"))
+        rough_root = sbuf("rough_root", [P, SLOTS * GROUPS], F32)
+        w_cols = sbuf("w_cols", [P, SLOTS * GROUPS], F32)
+        nc.scalar.activation(
+            out=rough_root[:].rearrange("p (t g) -> p t g", g=GROUPS), in_=w_turned[:, :, 0:GROUPS], func=ACT.Sqrt)
+        nc.scalar.copy(out=w_cols[:].rearrange("p (t g) -> p t g", g=GROUPS), in_=w_turned[:, :, 0:GROUPS])
+        ln_warm = sbuf("ln_warm", [P, SLOTS * GROUPS], F32)
+        nc.scalar.activation(out=ln_warm[:], in_=w_cols[:], func=ACT.Ln)
 
-        meg_grouped = gather_sensor("meg0", transpose_sensor("meg0", meg_raw[0], 0))
-        eeg_grouped = gather_sensor("eeg0", transpose_sensor("eeg0", eeg_raw[0], 2))
-        im_q[0] = quantize("inv_meg0", grouped)
-        half_quot = sbuf("half_quot", [P, 16], F32)
+        grouped = interleave_inv_meg(0)
+        inv_rough = sbuf("inv_rough", [P, SLOTS * GROUPS], F32)
+        nc.vector.reciprocal(out=inv_rough[:], in_=rough_root[:])
+        meg_grouped = turn_sensor("meg0", meg_raw[0], 0)
+        eeg_grouped = turn_sensor("eeg0", eeg_raw[0], 2)
+        inv_meg_q[0] = quantize("inv_meg0", grouped)
+        half_quotient = sbuf("half_quotient", [P, SLOTS * GROUPS], F32)
         nc.vector.scalar_tensor_tensor(
-            out=half_quot[:], in0=w_cols[:].rearrange("p t g -> p (t g)"), scalar=0.5, in1=inv_root[:], op0=ALU.mult, op1=ALU.mult)
-        nc.vector.tensor_copy(
-            out=f_scales[:].bitcast(I32).rearrange("p (g t m) -> p g t m", g=GROUPS, t=4),
-            in_=f_scales_raw[:].rearrange("p (g m t) -> p g t m", g=GROUPS, t=4))
-        root_w = sbuf("root_w", [P, 16], F32)
+            out=half_quotient[:], in0=w_cols[:], scalar=0.5, in1=inv_rough[:], op0=ALU.mult, op1=ALU.mult)
+        root_w = sbuf("root_w", [P, SLOTS * GROUPS], F32)
         nc.vector.scalar_tensor_tensor(
-            out=root_w[:], in0=root0[:].rearrange("p t g -> p (t g)"), scalar=0.5, in1=half_quot[:], op0=ALU.mult, op1=ALU.add)
+            out=root_w[:], in0=rough_root[:], scalar=0.5, in1=half_quotient[:], op0=ALU.mult, op1=ALU.add)
         meg_q[0] = quantize("meg0", meg_grouped)
-        sort_f_words(fw_first, 0, 1)
+        sort_f_words(f_words_first[:], 0, 1)
+        nc.vector.tensor_copy(
+            out=f_scales[:].bitcast(I32).rearrange("p (g t m) -> p g m t", g=GROUPS, t=SLOTS),
+            in_=f_scales_raw[:].rearrange("p (g m t) -> p g m t", g=GROUPS, t=SLOTS))
         eeg_q[0] = quantize("eeg0", eeg_grouped)
+        opened = [meg_pass(0, 0, t) for t in range(SLOTS)]
+        for t in range(SLOTS):
+            eeg_pass_and_square(0, 0, t, opened[t])
 
-        first = [meg_pass(0, 0, t) for t in range(4)]
-        for t in range(4):
-            eeg_pass(0, 0, t, first[t])
-            square(0, 0, t, first[t])
-
-        def power(h, g, copy):
-            return interleave_power("d%d%d" % (h, g), d_slots[h, g // 2][:, g % 2:g % 2 + 1], copy)
-
-        def quarter(c, gg, copy):
-            return interleave_power("dq%d%d" % (c, gg), d_slots[1, gg][:, :, :, 256 * c:256 * (c + 1)], copy)
-
-        a = interleave_inv_meg(1, on_vector)
-        sort_f_words(fw_rest, 1, GROUPS)
-        im_q[1] = quantize("inv_meg1", a)
+        grouped = interleave_inv_meg(1)
+        sort_f_words(f_words_rest[:, :K_PASS // 2], 1, 2)
+        inv_meg_q[1] = quantize("inv_meg1", grouped)
         currents(0, 1)
-        a = interleave_inv_meg(2, on_vector)
-        b = power(0, 0, on_vector)
-        im_q[2] = quantize("inv_meg2", a)
-        meg_grouped = gather_sensor("meg1", transpose_sensor("meg1", meg_raw[1], 0))
+        grouped = interleave_inv_meg(2)
+        d_grouped = first_half_power(0)
+        sort_f_words(f_words_rest[:, K_PASS // 2:], 2, GROUPS)
+        inv_meg_q[2] = quantize("inv_meg2", grouped)
+        meg_grouped = turn_sensor("meg1", meg_raw[1], 0)
         currents(0, 2)
-        a = interleave_inv_meg(3, on_vector)
-        d_q[0] = quantize("d00", b)
-        im_q[3] = quantize("inv_meg3", a)
-        eeg_grouped = gather_sensor("eeg1", transpose_sensor("eeg1", eeg_raw[1], 2))
+        grouped = interleave_inv_meg(3)
+        d_q[0] = quantize("d00", d_grouped)
+        inv_meg_q[3] = quantize("inv_meg3", grouped)
+        eeg_grouped = turn_sensor("eeg1", eeg_raw[1], 2)
         currents(0, 3)
-
-        b = power(0, 1, on_vector)
+        d_grouped = first_half_power(1)
         meg_q[1] = quantize("meg1", meg_grouped)
-        d_q[1] = quantize("d01", b)
+        d_q[1] = quantize("d01", d_grouped)
         eeg_q[1] = quantize("eeg1", eeg_grouped)
-        ps_cols = sbuf("ps_cols", [P, 4], F32)
-        gain_cols = sbuf("gain_cols", [P, 4], F32)
-        nc.scalar.copy(out=ps_cols[:], in_=ps_raw[:])
+        power_scale_cols = sbuf("power_scale_cols", [P, SLOTS], F32)
+        gain_cols = sbuf("gain_cols", [P, SLOTS], F32)
+        nc.scalar.copy(out=power_scale_cols[:], in_=power_scale_raw[:])
         nc.scalar.copy(out=gain_cols[:], in_=gain_raw[:])
         for g in range(GROUPS):
             currents(1, g)
 
         for g in range(2):
-            a = interleave_parcel_weights(g, on_vector)
-            b = power(0, g + 2, on_vector)
-            pw_q[g] = quantize("pw%d" % g, a)
-            d_q[g + 2] = quantize("d0%d" % (g + 2), b)
-        a = interleave_parcel_weights(2, on_vector)
-        b = interleave_parcel_weights(3, on_vector)
-        pw_q[2] = quantize("pw2", a)
-        a = quarter(0, 0, on_vector)
-        pw_q[3] = quantize("pw3", b)
-        qa0 = quantize("dq00", a)
-        late_a = quarter(0, 1, on_scalar)
+            grouped = interleave_parcel_weights(g)
+            d_grouped = first_half_power(g + 2)
+            pw_q[g] = quantize("pw%d" % g, grouped)
+            d_q[g + 2] = quantize("d0%d" % (g + 2), d_grouped)
+        grouped = interleave_parcel_weights(2)
+        last_grouped = interleave_parcel_weights(3)
+        pw_q[2] = quantize("pw2", grouped)
+        d_grouped = quarter_power(0, 0, on_vector)
+        pw_q[3] = quantize("pw3", last_grouped)
+        third_low = quantize("dq00", d_grouped)
+        third_high_grouped = quarter_power(0, 1, on_scalar)
 
-        half0, tok_a, tok_b = slice(0, 512), slice(512, 768), slice(768, 1024)
-        sums = [bank(u, "r0%d" % u, [P, HALF], F32) for u in range(4)]
+        half_banks = [bank(u, "r0%d" % u, [P, HALF], F32) for u in range(SLOTS)]
+        half_sums = [half_bank[:] for half_bank in half_banks]
         for g in range(GROUPS):
-            for u in range(4):
-                parcel_pass(sums[u][:], g, u, d_q[g])
-        for u in range(4):
-            logarithm(half0, u, sums[u][:])
-        a = quarter(1, 0, on_vector)
-        qa1 = quantize("dq01", late_a)
-        b = quarter(1, 1, on_vector)
-        for u in range(4):
-            gain_on_vector(half0, u)
-        qb0 = quantize("dq10", a)
-        qb1 = quantize("dq11", b)
+            for u in range(SLOTS):
+                parcel_pass(half_sums[u], g, u, *d_q[g])
+        logarithm(first_half, half_sums, range(SLOTS))
+        last_low_grouped = quarter_power(1, 0, on_vector)
+        third_high = quantize("dq01", third_high_grouped)
+        last_high_grouped = quarter_power(1, 1, on_vector)
+        apply_gain(first_half)
+        last_low = quantize("dq10", last_low_grouped)
+        last_high = quantize("dq11", last_high_grouped)
 
-        def columns(pair, g):
-            cols = slice(256 * (g % 2), 256 * (g % 2 + 1))
-            return pair[g // 2][0][:, cols], pair[g // 2][1][:, cols]
-
-        sums_a = [bank(4 + n, "ra%d" % n, [P, 2, 256], F32) for n in range(2)]
-        for u in range(4):
-            for g in range(GROUPS):
-                parcel_pass(sums_a[u // 2][:, u % 2, :], g, u, columns((qa0, qa1), g))
-        transpose_y(half0, 0)
-        for u in range(4):
-            logarithm(tok_a, u, sums_a[u // 2][:, u % 2, :])
-        sums_b = [bank(6 + n, "rb%d" % n, [P, 2, 256], F32) for n in range(2)]
-        for u in range(4):
-            for g in range(GROUPS):
-                parcel_pass(sums_b[u // 2][:, u % 2, :], g, u, columns((qb0, qb1), g))
-        for u in range(4):
-            gain_on_vector(tok_a, u)
-        y_grouped = interleave_y(half0)
+        third_sums = quarter_passes(4, (third_low, third_high))
+        transpose_y(first_half, 0)
+        logarithm(third_quarter, third_sums, range(SLOTS))
+        last_sums = quarter_passes(6, (last_low, last_high))
+        apply_gain(third_quarter)
+        half_y = interleave_y(first_half)
         for i in range(3):
             store_y(i, on_scalar)
-        transpose_y(tok_a, 4)
-        for u in range(4):
-            logarithm(tok_b, u, sums_b[u // 2][:, u % 2, :])
-        y_grouped_a = interleave_y(tok_a)
-        store_y_codes(half0, y_grouped)
+        transpose_y(third_quarter, 4)
+        logarithm(last_quarter, last_sums, range(2))
         store_y(3, on_scalar)
-        for u in range(4):
-            gain_on_vector(tok_b, u)
-        for i in range(4, 6):
-            store_y(i, on_scalar)
-        store_y_codes(tok_a, y_grouped_a)
-        transpose_y(tok_b, 6)
-        y_grouped = interleave_y(tok_b)
+        logarithm(last_quarter, last_sums, range(2, SLOTS))
+        third_y = interleave_y(third_quarter)
+        quantize_y(first_half, half_y)
+        store_y_codes(first_half)
+        apply_gain(last_quarter)
+        store_y(4, on_scalar)
+        store_y(5, on_scalar)
+        quantize_y(third_quarter, third_y)
+        transpose_y(last_quarter, 6)
+        last_y = interleave_y(last_quarter)
         store_y(6, on_scalar)
-        store_y_codes(tok_b, y_grouped)
         store_y(7, on_vector)
-        store_y_scales(slice(0, T), nc.sync)
+        quantize_y(last_quarter, last_y)
+        store_y_codes(slice(HALF, SAMPLES))
+        for quad in range(4):
+            nc.sync.dma_start(
+                out=out_2[0, 4 * quad:4 * quad + 4, :].bitcast(I32),
+                in_=y_scales[32 * quad:32 * quad + 4, :].bitcast(I32))

from contextlib import ExitStack

import concourse.mybir as mybir
from concourse.masks import make_identity

SAMPLES, CHANNELS, SOURCES, PARCELS = 1024, 512, 2048, 512
FLOPS = 2 * SAMPLES * (2 * CHANNELS * SOURCES + SOURCES * PARCELS)

F32 = mybir.dt.float32
BF16 = mybir.dt.bfloat16
I32 = mybir.dt.int32
U32 = mybir.dt.uint32
U8 = mybir.dt.uint8
FP8X4 = mybir.dt.float8_e4m3fn_x4
FP4X4 = mybir.dt.float4_e2m1fn_x4
ACT = mybir.ActivationFunctionType
ALU = mybir.AluOpType

P = 128
SLOTS = 4
K_PASS = P * SLOTS
GROUPS = SOURCES // K_PASS
HALF = 512
QUARTER = 256
STAGING_BUFS = 5
ROW_BUFS = 6


def tile_minimum_norm_parcel_power_k6_kernel(
    tc, eeg, meg, inv_eeg_words, inv_eeg_scales, inv_meg, source_weight, parcel_weights,
    power_scale, gain, out_0, out_1, out_2
):
    nc = tc.nc
    with ExitStack() as ctx:
        sb = ctx.enter_context(tc.tile_pool(name="sb", bufs=1))
        ps = ctx.enter_context(tc.psum_pool(name="ps", bufs=1))
        ctx.enter_context(tc.manual_schedule())
        on_vector, on_scalar = nc.vector.tensor_copy, nc.scalar.copy

        def sbuf(name, shape, dtype):
            return sb.tile(shape, dtype, name=name, align_bytes=64)

        def staging(name):
            return sb.tile([P, SLOTS * K_PASS], BF16, name=name, tag="staging", bufs=STAGING_BUFS, align_bytes=64)

        def bank(number, name, shape, dtype):
            return ps.tile(shape, dtype, name=name, tag="bank%d" % number)

        w_rows = sbuf("w_rows", [P, K_PASS], BF16)
        nc.vector.memset(w_rows[:], 0.0)
        f_scales_raw = sbuf("f_scales_raw", [P, SOURCES // 4], I32)
        nc.vector.memset(f_scales_raw[:], 0)
        ident16 = sbuf("ident16", [P, P], BF16)
        make_identity(nc, ident16[:])
        ident32 = sbuf("ident32", [P, P], F32)
        make_identity(nc, ident32[:])

        def load_inv_meg(g):
            raw = sbuf("inv_meg_raw%d" % g, [P, SLOTS, K_PASS], BF16)
            cols = inv_meg[:, K_PASS * g:K_PASS * (g + 1)]
            nc.sync.dma_start(out=raw[:], in_=cols.rearrange("(p j) n -> p j n", j=SLOTS))
            return raw

        def load_sensor_quarters(name, x):
            quarters = []
            for c in range(2):
                raw = sbuf("%s_raw0%d" % (name, c), [P, 2 * CHANNELS], BF16)
                rows = x[QUARTER * c:QUARTER * (c + 1), :]
                nc.sync.dma_start(out=raw[:], in_=rows.rearrange("(p i) k -> p (i k)", i=2))
                quarters.append(raw[:])
            return quarters

        def load_sensor_half(name, x):
            raw = sbuf("%s_raw1" % name, [P, 4 * CHANNELS], BF16)
            nc.sync.dma_start(
                out=raw[:].rearrange("p (c k) -> p c k", c=2),
                in_=x[HALF:, :].rearrange("(c p i) k -> p c (i k)", c=2, i=2))
            return [raw[:, 2 * CHANNELS * c:2 * CHANNELS * (c + 1)] for c in range(2)]

        def load_f_words(g0, g1):
            raw = sbuf("f_words_raw%d" % g0, [P, K_PASS // 2 * (g1 - g0)], I32)
            nc.sync.dma_start(out=raw[:], in_=inv_eeg_words[0, :, 2 * K_PASS * g0:2 * K_PASS * g1].bitcast(I32))
            return raw

        def load_parcel_weights(g):
            raw = sbuf("pw_raw%d" % g, [P, SLOTS, PARCELS], BF16)
            rows = parcel_weights[K_PASS * g:K_PASS * (g + 1), :].rearrange("(m t e) n -> t m e n", t=SLOTS, e=4)
            for t in range(SLOTS):
                nc.sync.dma_start(out=raw[:, t, :], in_=rows[t])
            return raw

        def load_parcel_vector(name, vec):
            raw = sbuf(name, [P, SLOTS], BF16)
            nc.sync.dma_start(out=raw[:], in_=vec.rearrange("(p u) -> p u", u=SLOTS))
            return raw

        inv_meg_raw, meg_raw, eeg_raw = {}, {}, {}
        w_raw = sbuf("w_raw", [GROUPS, K_PASS], BF16)
        nc.sync.dma_start(out=w_raw[:], in_=source_weight.rearrange("(g s) -> g s", g=GROUPS))
        inv_meg_raw[0] = load_inv_meg(0)
        meg_raw[0] = load_sensor_quarters("meg", meg)
        eeg_raw[0] = load_sensor_quarters("eeg", eeg)
        f_words_first = load_f_words(0, 1)
        for quad in range(4):
            nc.sync.dma_start(
                out=f_scales_raw[32 * quad:32 * quad + 4, :],
                in_=inv_eeg_scales[0, 4 * quad:4 * quad + 4, :].bitcast(I32))
        inv_meg_raw[1] = load_inv_meg(1)
        f_words_rest = load_f_words(1, GROUPS)
        inv_meg_raw[2] = load_inv_meg(2)
        meg_raw[1] = load_sensor_half("meg", meg)
        inv_meg_raw[3] = load_inv_meg(3)
        eeg_raw[1] = load_sensor_half("eeg", eeg)
        power_scale_raw = load_parcel_vector("power_scale_raw", power_scale)
        gain_raw = load_parcel_vector("gain_raw", gain)
        pw_raw = [load_parcel_weights(g) for g in range(GROUPS)]

        def quantize(name, grouped):
            codes = sbuf(name + "_codes", [P, K_PASS], U32)
            scales = sbuf(name + "_scales", [P, K_PASS], U8)
            nc.vector.quantize_mx(out=codes[:].bitcast(FP8X4), scales=scales[:], in_=grouped[:])
            return codes[:], scales[:]

        def interleave_inv_meg(g):
            grouped = staging("inv_meg_grouped%d" % g)
            nc.vector.tensor_copy(
                out=grouped[:].rearrange("p (t m e j) -> p m t j e", t=SLOTS, e=4, j=SLOTS),
                in_=inv_meg_raw[g][:].rearrange("p j (m t e) -> p m t j e", t=SLOTS, e=4))
            return grouped

        def interleave_parcel_weights(g):
            grouped = staging("pw_grouped%d" % g)
            nc.vector.tensor_copy(
                out=grouped[:].rearrange("p (u n t) -> p n t u", u=SLOTS, t=SLOTS),
                in_=pw_raw[g][:].rearrange("p t (n u) -> p n t u", u=SLOTS))
            return grouped

        def interleave_power(name, slots, copy):
            grouped = staging(name + "_grouped")
            copy(
                out=grouped[:].rearrange("p (g r i t) -> p g r t i", g=slots.shape[1], i=4, t=SLOTS),
                in_=slots.rearrange("p g t (r i) -> p g r t i", i=4))
            return grouped

        def turn_sensor(name, quarters, first_bank):
            turned = []
            for c in range(2):
                both = bank(first_bank + c, "%s_turned%d" % (name, c), [P, 2, 2, P], F32)
                words = quarters[c].bitcast(F32)
                for i in range(2):
                    for w in range(2):
                        row_words = words[:, CHANNELS // 2 * i + w:CHANNELS // 2 * (i + 1):2]
                        nc.tensor.transpose(both[:, i, w, :], row_words, ident32[:])
                turned.append(both)
            grouped = sbuf(name + "_grouped", [P, SLOTS * HALF], BF16)
            grouped_words = grouped[:].bitcast(F32).rearrange("p (c r i w) -> p c r i w", c=2, i=2, w=2)
            for c in range(2):
                nc.scalar.copy(out=grouped_words[:, c], in_=turned[c][:].rearrange("p i w r -> p r i w"))
            return grouped

        f_words = sbuf("f_words", [P, 2 * SOURCES], U8)
        f_scales = sbuf("f_scales", [P, SOURCES], U8)

        def sort_f_words(raw, g0, g1):
            sorted_words = f_words[:, 2 * K_PASS * g0:2 * K_PASS * g1].bitcast(I32)
            nc.vector.tensor_copy(
                out=sorted_words.rearrange("p (g t m x) -> p g m t x", t=SLOTS, m=32, x=2),
                in_=raw.rearrange("p (g m t x) -> p g m t x", t=SLOTS, m=32, x=2))

        inv_meg_q, meg_q, eeg_q = {}, {}, {}
        d_slots = {}
        for h in range(2):
            for pair in range(GROUPS // 2):
                d_slots[h, pair] = sbuf("d_slots%d%d" % (h, pair), [P, 2, SLOTS, HALF], BF16)

        def meg_pass(h, g, t):
            current = bank(4 + t, "j%d%d%d" % (h, g, t), [P, HALF], F32)
            codes, scales = inv_meg_q[g]
            cols = slice(P * t, P * (t + 1))
            nc.tensor.matmul_mx(
                out=current[:], lhsT=codes[:, cols].bitcast(FP8X4), lhsT_scale=scales[:, cols],
                rhs=meg_q[h][0].bitcast(FP8X4), rhs_scale=meg_q[h][1], start=True, stop=False)
            return current

        def eeg_pass_and_square(h, g, t, current):
            c0 = K_PASS * g + P * t
            nc.tensor.matmul_mx(
                out=current[:], lhsT=f_words[:, 2 * c0:2 * (c0 + P)].bitcast(FP4X4), lhsT_scale=f_scales[:, c0:c0 + P],
                rhs=eeg_q[h][0].bitcast(FP8X4), rhs_scale=eeg_q[h][1], start=False, stop=True)
            nc.scalar.activation(
                out=d_slots[h, g // 2][:, g % 2, t, :], in_=current[:], func=ACT.Square,
                scale=root_w[:, GROUPS * t + g:GROUPS * t + g + 1])

        def currents(h, g):
            for t in range(SLOTS):
                eeg_pass_and_square(h, g, t, meg_pass(h, g, t))

        def first_half_power(g):
            return interleave_power("d0%d" % g, d_slots[0, g // 2][:, g % 2:g % 2 + 1], on_vector)

        def quarter_power(c, pair, copy):
            slots = d_slots[1, pair][:, :, :, QUARTER * c:QUARTER * (c + 1)]
            return interleave_power("dq%d%d" % (c, pair), slots, copy)

        pw_q, d_q, y_banks, logs, y_slots = {}, {}, {}, {}, {}
        first_half = slice(0, HALF)
        third_quarter = slice(HALF, HALF + QUARTER)
        last_quarter = slice(HALF + QUARTER, SAMPLES)
        for span in (first_half, third_quarter, last_quarter):
            logs[span.start] = sbuf("logs%d" % span.start, [P, SLOTS, span.stop - span.start], F32)
            y_slots[span.start] = sbuf("y_slots%d" % span.start, [P, SLOTS, span.stop - span.start], F32)
        y_codes = sbuf("y_codes", [P, SAMPLES], U32)
        y_scales = sbuf("y_scales", [P, SAMPLES], U8)

        def parcel_pass(out, g, u, power_codes, power_scales):
            codes, scales = pw_q[g]
            cols = slice(P * u, P * (u + 1))
            nc.tensor.matmul_mx(
                out=out, lhsT=codes[:, cols].bitcast(FP8X4), lhsT_scale=scales[:, cols],
                rhs=power_codes.bitcast(FP8X4), rhs_scale=power_scales, start=(g == 0), stop=(g == GROUPS - 1))

        def quarter_passes(first_bank, pairs):
            banks = [bank(first_bank + n, "rq%d" % (first_bank + n), [P, 2, QUARTER], F32) for n in range(2)]
            sums = [banks[u // 2][:, u % 2, :] for u in range(SLOTS)]
            for u in range(SLOTS):
                for g in range(GROUPS):
                    codes, scales = pairs[g // 2]
                    cols = slice(QUARTER * (g % 2), QUARTER * (g % 2 + 1))
                    parcel_pass(sums[u], g, u, codes[:, cols], scales[:, cols])
            return sums

        def logarithm(span, sums, parcel_slots):
            for u in parcel_slots:
                nc.scalar.activation(
                    out=logs[span.start][:, u, :], in_=sums[u], func=ACT.Ln,
                    scale=power_scale_cols[:, u:u + 1], bias=1.0)

        def apply_gain(span):
            for u in range(SLOTS):
                nc.vector.tensor_scalar(
                    out=y_slots[span.start][:, u, :], in0=logs[span.start][:, u, :],
                    scalar1=gain_cols[:, u:u + 1], scalar2=None, op0=ALU.mult)

        def transpose_y(span, first_bank):
            tiles = range(span.start // P, span.stop // P)
            for n, i in enumerate(tiles):
                y_banks[i] = bank(first_bank + n, "yt%d" % i, [P, SLOTS, P], F32)
            for u in range(SLOTS):
                for n, i in enumerate(tiles):
                    nc.tensor.transpose(y_banks[i][:, u, :], y_slots[span.start][:, u, P * n:P * (n + 1)], ident32[:])

        def store_y(i, copy):
            rows = sb.tile([P, PARCELS], F32, name="y_rows%d" % i, tag="y_rows", bufs=ROW_BUFS, align_bytes=64)
            copy(out=rows[:].rearrange("p (n u) -> p n u", u=SLOTS), in_=y_banks[i][:].rearrange("p u n -> p n u"))
            nc.sync.dma_start(out=out_0[P * i:P * (i + 1), :], in_=rows[:])

        def interleave_y(span):
            grouped = staging("y_grouped%d" % span.start)
            part = grouped[:, 0:SLOTS * (span.stop - span.start)]
            nc.vector.tensor_copy(
                out=part.rearrange("p (r i u) -> p r u i", i=4, u=SLOTS),
                in_=y_slots[span.start][:].rearrange("p u (r i) -> p r u i", i=4))
            return part

        def quantize_y(span, grouped):
            nc.vector.quantize_mx(out=y_codes[:, span].bitcast(FP8X4), scales=y_scales[:, span], in_=grouped)

        def store_y_codes(span):
            nc.sync.dma_start(
                out=out_1[0, :, span, :].rearrange("p n u -> p (n u)").bitcast(I32), in_=y_codes[:, span].bitcast(I32))

        nc.vector.tensor_copy(
            out=w_rows[0:GROUPS, :].rearrange("g (t m e) -> g m t e", t=SLOTS, e=4),
            in_=w_raw[:].rearrange("g (m t e) -> g m t e", t=SLOTS, e=4))
        w_turned = bank(7, "w_turned", [P, SLOTS, P], BF16)
        for t in range(SLOTS):
            nc.tensor.transpose(w_turned[:, t, :], w_rows[:, P * t:P * (t + 1)], ident16[:])
        rough_root = sbuf("rough_root", [P, SLOTS * GROUPS], F32)
        w_cols = sbuf("w_cols", [P, SLOTS * GROUPS], F32)
        nc.scalar.activation(
            out=rough_root[:].rearrange("p (t g) -> p t g", g=GROUPS), in_=w_turned[:, :, 0:GROUPS], func=ACT.Sqrt)
        nc.scalar.copy(out=w_cols[:].rearrange("p (t g) -> p t g", g=GROUPS), in_=w_turned[:, :, 0:GROUPS])
        ln_warm = sbuf("ln_warm", [P, SLOTS * GROUPS], F32)
        nc.scalar.activation(out=ln_warm[:], in_=w_cols[:], func=ACT.Ln)

        grouped = interleave_inv_meg(0)
        inv_rough = sbuf("inv_rough", [P, SLOTS * GROUPS], F32)
        nc.vector.reciprocal(out=inv_rough[:], in_=rough_root[:])
        meg_grouped = turn_sensor("meg0", meg_raw[0], 0)
        eeg_grouped = turn_sensor("eeg0", eeg_raw[0], 2)
        inv_meg_q[0] = quantize("inv_meg0", grouped)
        half_quotient = sbuf("half_quotient", [P, SLOTS * GROUPS], F32)
        nc.vector.scalar_tensor_tensor(
            out=half_quotient[:], in0=w_cols[:], scalar=0.5, in1=inv_rough[:], op0=ALU.mult, op1=ALU.mult)
        root_w = sbuf("root_w", [P, SLOTS * GROUPS], F32)
        nc.vector.scalar_tensor_tensor(
            out=root_w[:], in0=rough_root[:], scalar=0.5, in1=half_quotient[:], op0=ALU.mult, op1=ALU.add)
        meg_q[0] = quantize("meg0", meg_grouped)
        sort_f_words(f_words_first[:], 0, 1)
        nc.vector.tensor_copy(
            out=f_scales[:].bitcast(I32).rearrange("p (g t m) -> p g m t", g=GROUPS, t=SLOTS),
            in_=f_scales_raw[:].rearrange("p (g m t) -> p g m t", g=GROUPS, t=SLOTS))
        eeg_q[0] = quantize("eeg0", eeg_grouped)
        opened = [meg_pass(0, 0, t) for t in range(SLOTS)]
        for t in range(SLOTS):
            eeg_pass_and_square(0, 0, t, opened[t])

        grouped = interleave_inv_meg(1)
        sort_f_words(f_words_rest[:, :K_PASS // 2], 1, 2)
        inv_meg_q[1] = quantize("inv_meg1", grouped)
        currents(0, 1)
        grouped = interleave_inv_meg(2)
        d_grouped = first_half_power(0)
        sort_f_words(f_words_rest[:, K_PASS // 2:], 2, GROUPS)
        inv_meg_q[2] = quantize("inv_meg2", grouped)
        meg_grouped = turn_sensor("meg1", meg_raw[1], 0)
        currents(0, 2)
        grouped = interleave_inv_meg(3)
        d_q[0] = quantize("d00", d_grouped)
        inv_meg_q[3] = quantize("inv_meg3", grouped)
        eeg_grouped = turn_sensor("eeg1", eeg_raw[1], 2)
        currents(0, 3)
        d_grouped = first_half_power(1)
        meg_q[1] = quantize("meg1", meg_grouped)
        d_q[1] = quantize("d01", d_grouped)
        eeg_q[1] = quantize("eeg1", eeg_grouped)
        power_scale_cols = sbuf("power_scale_cols", [P, SLOTS], F32)
        gain_cols = sbuf("gain_cols", [P, SLOTS], F32)
        nc.scalar.copy(out=power_scale_cols[:], in_=power_scale_raw[:])
        nc.scalar.copy(out=gain_cols[:], in_=gain_raw[:])
        for g in range(GROUPS):
            currents(1, g)

        for g in range(2):
            grouped = interleave_parcel_weights(g)
            d_grouped = first_half_power(g + 2)
            pw_q[g] = quantize("pw%d" % g, grouped)
            d_q[g + 2] = quantize("d0%d" % (g + 2), d_grouped)
        grouped = interleave_parcel_weights(2)
        last_grouped = interleave_parcel_weights(3)
        pw_q[2] = quantize("pw2", grouped)
        d_grouped = quarter_power(0, 0, on_vector)
        pw_q[3] = quantize("pw3", last_grouped)
        third_low = quantize("dq00", d_grouped)
        third_high_grouped = quarter_power(0, 1, on_scalar)

        half_banks = [bank(u, "r0%d" % u, [P, HALF], F32) for u in range(SLOTS)]
        half_sums = [half_bank[:] for half_bank in half_banks]
        for g in range(GROUPS):
            for u in range(SLOTS):
                parcel_pass(half_sums[u], g, u, *d_q[g])
        logarithm(first_half, half_sums, range(SLOTS))
        last_low_grouped = quarter_power(1, 0, on_vector)
        third_high = quantize("dq01", third_high_grouped)
        last_high_grouped = quarter_power(1, 1, on_vector)
        apply_gain(first_half)
        last_low = quantize("dq10", last_low_grouped)
        last_high = quantize("dq11", last_high_grouped)

        third_sums = quarter_passes(4, (third_low, third_high))
        transpose_y(first_half, 0)
        logarithm(third_quarter, third_sums, range(SLOTS))
        last_sums = quarter_passes(6, (last_low, last_high))
        apply_gain(third_quarter)
        half_y = interleave_y(first_half)
        for i in range(3):
            store_y(i, on_scalar)
        transpose_y(third_quarter, 4)
        logarithm(last_quarter, last_sums, range(2))
        store_y(3, on_scalar)
        logarithm(last_quarter, last_sums, range(2, SLOTS))
        third_y = interleave_y(third_quarter)
        quantize_y(first_half, half_y)
        store_y_codes(first_half)
        apply_gain(last_quarter)
        store_y(4, on_scalar)
        store_y(5, on_scalar)
        quantize_y(third_quarter, third_y)
        transpose_y(last_quarter, 6)
        last_y = interleave_y(last_quarter)
        store_y(6, on_scalar)
        store_y(7, on_vector)
        quantize_y(last_quarter, last_y)
        store_y_codes(slice(HALF, SAMPLES))
        for quad in range(4):
            nc.sync.dma_start(
                out=out_2[0, 4 * quad:4 * quad + 4, :].bitcast(I32),
                in_=y_scales[32 * quad:32 * quad + 4, :].bitcast(I32))
